import numpy as np
import ml_dtypes


def mxq(x, axis, fmt="e4m3"):
    dtype, down = {"e4m3": (ml_dtypes.float8_e4m3fn, 7), "e5m2": (ml_dtypes.float8_e5m2, 14)}[fmt]
    v = np.moveaxis(np.asarray(x, np.float32).astype(ml_dtypes.bfloat16).astype(np.float64), axis, -1)
    blocks = v.reshape(v.shape[:-1] + (-1, 32))
    amax = np.abs(blocks).max(-1, keepdims=True)
    byte = np.maximum(np.where(amax > 0, np.frexp(amax)[1] - 1 + 127, 0) - down, 1)
    scale = np.exp2(byte - 127.0)
    codes = (blocks / scale).astype(np.float32).astype(dtype).astype(np.float64)
    return np.moveaxis((codes * scale).reshape(v.shape), -1, axis)


WIDE = False


def mx_kscale(k):
    if not WIDE:
        return np.ones(k)
    levels = np.array([10, -10, 5, -5, 0])
    if k % 512:
        return np.exp2(np.random.permutation(np.resize(levels, k // 32))).repeat(32)
    a = np.empty((k // 512, 16))
    for p in range(k // 512):
        a[p, :8] = np.random.permutation(np.resize(levels, 8))
        for g in range(8):
            far = levels[np.abs(levels - a[p, g]) >= 10]
            a[p, g + 8] = far[np.random.randint(len(far))]
    return np.exp2(a.ravel()).repeat(32)


def f64(x):
    return np.asarray(x).astype(np.float64)


def striped(idx):
    return np.tile(idx.reshape(-1, 16).T, (8, 1)).astype(np.uint16)


def unstriped(offs):
    return offs[:16].T.reshape(-1).astype(np.int64)


E2M1 = np.array([0.0, 0.5, 1.0, 1.5, 2.0, 3.0, 4.0, 6.0, -0.0, -0.5, -1.0, -1.5, -2.0, -3.0, -4.0, -6.0])


def pack_weight(w, fmt):
    k, n = w.shape
    w = f64(np.asarray(w, np.float32).astype(ml_dtypes.bfloat16)).reshape(k // 32, 32, n)
    amax = np.abs(w).max(1)
    if fmt == "e4m3":
        byte = np.frexp(amax)[1] - 1 + 127 - 7
    else:
        mant, ex = np.frexp(amax / 6.0)
        byte = np.where(mant > 0.5, ex, ex - 1) + 127
    byte = np.clip(np.where(amax > 0, byte, 1), 1, 254)
    scaled = (w * np.exp2(127.0 - byte)[:, None, :]).reshape(k, n).astype(np.float32)
    by_word = np.ascontiguousarray(scaled.reshape(k // 512, 128, 4, n).transpose(0, 1, 3, 2))
    if fmt == "e4m3":
        words = by_word.astype(ml_dtypes.float8_e4m3fn).view(np.uint8)
    else:
        c = by_word.astype(ml_dtypes.float4_e2m1fn).view(np.uint8) & 0xF
        words = (c[..., 0::2] | (c[..., 1::2] << 4)).reshape(k // 512, 128, 2 * n)
    return np.ascontiguousarray(words), np.ascontiguousarray(byte.astype(np.uint8).reshape(k // 512, 16, n))


def unpack_weight(words, scales, fmt):
    g, _, n = scales.shape
    words = np.ascontiguousarray(words).reshape(g, 128, n, -1)
    if fmt == "e4m3":
        vals = words.view(ml_dtypes.float8_e4m3fn).astype(np.float64)
    else:
        nib = np.empty((g, 128, n, 4), np.uint8)
        nib[..., 0::2] = words & 0xF
        nib[..., 1::2] = words >> 4
        vals = E2M1[nib]
    vals = vals * np.repeat(np.exp2(scales.astype(np.float64) - 127.0), 8, axis=1)[..., None]
    return vals.transpose(0, 1, 3, 2).reshape(g * 512, n)


def gelu(v):
    return 0.5 * v * (1.0 + np.tanh(np.sqrt(2.0 / np.pi) * (v + 0.044715 * v**3)))


def bf(x):
    return np.asarray(x, np.float32).astype(ml_dtypes.bfloat16)


def planes(Y):
    n, m = Y.shape
    b = f64(bf(Y)).reshape(n // 32, 32, m)
    amax = np.abs(b).max(1)
    byte = np.clip(np.where(amax > 0, np.frexp(amax)[1] - 1 + 127 - 7, 1), 1, 254)
    codes = (b * np.exp2(127.0 - byte)[:, None, :]).reshape(n, m).astype(np.float32).astype(ml_dtypes.float8_e4m3fn).view(np.uint8)
    words = codes.reshape(n // 512, 128, 4, m).transpose(0, 1, 3, 2)
    return np.ascontiguousarray(words), np.ascontiguousarray(byte.astype(np.uint8).reshape(n // 512, 16, m))


K, H, N, T, S = 1024, 512, 256, 2048, 1024


def setup_inputs():
    n = np.random.standard_normal
    s = mx_kscale(K)[:, None]
    u = mx_kscale(H)[:, None]
    tab_words, tab_scales = pack_weight(n((K, T)) * s, "e4m3")
    w2_words, w2_scales = pack_weight(n((K, H)) / np.sqrt(K) / s, "e2m1")
    w3_words, w3_scales = pack_weight(0.7 * n((K, H)) / np.sqrt(K) / s * u.T, "e4m3")
    w5_words, w5_scales = pack_weight(n((H, N)) / np.sqrt(H) / u, "e2m1")
    return {
        "tab_words": tab_words, "tab_scales": tab_scales,
        "offs": striped(np.random.permutation(T)[:S]),
        "w1": (1.5 * n((K, H)) / np.sqrt(K) / s * u.T).astype(np.float32),
        "w2_words": w2_words, "w2_scales": w2_scales,
        "w3_words": w3_words, "w3_scales": w3_scales,
        "w4": (n((H, N)) / np.sqrt(H) / u).astype(np.float32),
        "w5_words": w5_words, "w5_scales": w5_scales,
        "ded": np.random.uniform(0.2, 1.5, (N, S)).astype(np.float32),
    }


def reference(tab_words, tab_scales, offs, w1, w2_words, w2_scales, w3_words, w3_scales, w4, w5_words, w5_scales, ded):
    v = unpack_weight(tab_words, tab_scales, "e4m3")[:, unstriped(offs)]
    a = mxq(f64(w1), 0, "e4m3").T @ v
    b = unpack_weight(w2_words, w2_scales, "e2m1").T @ v
    c = unpack_weight(w3_words, w3_scales, "e4m3").T @ v
    h = a / (1.0 + b * b) + c
    words, scales = planes(h)
    hq = mxq(h, 0, "e4m3")
    y1 = mxq(f64(w4), 0, "e4m3").T @ hq
    y2 = unpack_weight(w5_words, w5_scales, "e2m1").T @ hq
    y = np.maximum(y1, y2) - f64(ded)
    return y, h, words, scales

@@ -1,0 +1,283 @@
+from contextlib import ExitStack
+
+import concourse.mybir as mybir
+
+K, H, N, T, S = 1024, 512, 256, 2048, 1024
+FLOPS = 2 * S * H * (3 * K + 2 * N)
+
+F32 = mybir.dt.float32
+BF16 = mybir.dt.bfloat16
+I32 = mybir.dt.int32
+U32 = mybir.dt.uint32
+U16 = mybir.dt.uint16
+U8 = mybir.dt.uint8
+FP8X4 = mybir.dt.float8_e4m3fn_x4
+FP4X4 = mybir.dt.float4_e2m1fn_x4
+ACT = mybir.ActivationFunctionType
+ALU = mybir.AluOpType
+
+P = 128
+PACK = 4
+PASSES = K // (P * PACK)
+QUADS = 4
+CHUNK = 512
+CHUNKS = S // CHUNK
+UNIT = 256
+UNITS = S // UNIT
+PAIRS = PACK // 2
+GROUPS = N // P
+
+
+def tile_list_crop_index_payout_kernel(
+    tc, tab_words, tab_scales, offs, w1, w2_words, w2_scales, w3_words, w3_scales, w4, w5_words, w5_scales, ded,
+    out_0, out_1, out_2, out_3,
+):
+    nc = tc.nc
+    with ExitStack() as ctx:
+        keep = ctx.enter_context(tc.tile_pool(name="keep", bufs=1))
+        ring = ctx.enter_context(tc.tile_pool(name="ring", bufs=2))
+        psum = ctx.enter_context(tc.psum_pool(name="psum", bufs=2))
+
+        offsets = keep.tile([P, S // 16], U16, name="offsets")
+        tab_w = [keep.tile([P, T], I32, name="tab_w%d" % a, tag="slot_tab_w%d" % a, align_bytes=64) for a in range(PASSES)]
+        tab_s = keep.tile([P, T], U8, name="tab_s", tag="slot_tab_s", align_bytes=64)
+        v_w = [keep.tile([P, PASSES * CHUNK], U32, name="v_w0", align_bytes=64)]
+        picked_s = keep.tile([P, S], U8, name="picked_s", align_bytes=64)
+        v_s = keep.tile([P, PASSES * S], U8, name="v_s", align_bytes=64)
+        w1_bf = [keep.tile([P, PACK * H], BF16, name="w1_bf%d" % a, align_bytes=64) for a in range(PASSES)]
+        w1_w = [keep.tile([P, H], U32, name="w1_w%d" % a, align_bytes=64) for a in range(PASSES)]
+        w1_s = [keep.tile([P, H], U8, name="w1_s%d" % a, align_bytes=64) for a in range(PASSES)]
+        w2_raw = keep.tile([P, PASSES * 2 * H], U8, name="w2_raw", tag="slot_w2", align_bytes=64)
+        w2_w = keep.tile([P, PASSES * 2 * H], U8, name="w2_w", align_bytes=64)
+        w3_w = keep.tile([P, PASSES * H], I32, name="w3_w", align_bytes=64)
+        w2_s_raw = keep.tile([P, PASSES * H], U8, name="w2_s_raw", tag="slot_w2_s", align_bytes=64)
+        w3_s_raw = keep.tile([P, H], U8, name="w3_s_raw", align_bytes=64)
+        w5_s = keep.tile([P, N], U8, name="w5_s", align_bytes=64)
+        w2_s = keep.tile([P, PASSES * H], U8, name="w2_s", align_bytes=64)
+        w3_s = keep.tile([P, H], U8, name="w3_s", align_bytes=64)
+        w4_bf = keep.tile([P, PACK * N], BF16, name="w4_bf", align_bytes=64)
+        w4_w = keep.tile([P, N], U32, name="w4_w", align_bytes=64)
+        w4_s = keep.tile([P, N], U8, name="w4_s", align_bytes=64)
+        out_1_rows = out_1.rearrange("(p t) s -> p t s", t=PACK)
+        out_0_rows = out_0.rearrange("(g p) s -> p g s", p=P)
+        h_w = keep.tile([P, S], U32, name="h_w", align_bytes=64)
+        h_s = keep.tile([P, S], U8, name="h_s", align_bytes=64)
+        warm = keep.tile([P, 1], F32, name="warm")
+        warm_out = keep.tile([P, 1], F32, name="warm_out")
+
+        for plane in (w2_s_raw[:], tab_s[32:64, :], tab_s[64:P, :]):
+            nc.vector.memset(plane.bitcast(I32), 0)
+        nc.vector.memset(warm[:], 1.0)
+        for plane in (v_s, w3_s_raw, w5_s):
+            nc.gpsimd.memset(plane[:].bitcast(I32), 0)
+        for q in range(QUADS):
+            nc.gpsimd.dma_start(out=w3_s_raw[32 * q : 32 * q + 8, :].bitcast(I32), in_=w3_scales[:, 4 * q : 4 * q + 4, :].bitcast(I32))
+        for q in range(QUADS):
+            nc.gpsimd.dma_start(out=w5_s[32 * q : 32 * q + 4, :].bitcast(I32), in_=w5_scales[0, 4 * q : 4 * q + 4, :].bitcast(I32))
+
+        def words(dram, a):
+            return dram[a].rearrange("p e i -> p (e i)").bitcast(I32)
+
+        nc.sync.dma_start(offsets[:], offs)
+        nc.sync.dma_start(out=tab_s[0:32, :].bitcast(I32), in_=tab_scales.rearrange("a q t -> (a q) t").bitcast(I32))
+        nc.sync.dma_start(out=tab_w[0][:], in_=words(tab_words, 0))
+        nc.sync.dma_start(
+            out=w2_raw[:].bitcast(I32).rearrange("p (a e) -> p a e", a=PASSES), in_=w2_words.bitcast(I32).rearrange("a p e -> p a e")
+        )
+        nc.sync.dma_start(out=tab_w[1][:], in_=words(tab_words, 1))
+        for q in range(QUADS):
+            nc.scalar.dma_start(
+                out=w2_s_raw[32 * q : 32 * q + 4, :].bitcast(I32).rearrange("r (a e) -> r a e", a=PASSES),
+                in_=w2_scales.bitcast(I32)[:, 4 * q : 4 * q + 4, :].rearrange("a r e -> r a e"),
+            )
+        nc.scalar.activation(warm_out[:], warm[:], ACT.Abs_reciprocal_sqrt)
+        w1_raw = []
+
+        def load_w1(a, slot):
+            raw = keep.tile([P, PACK, H], F32, name="w1_raw%d" % a, tag=slot, align_bytes=64)
+            nc.sync.dma_start(out=raw[:], in_=w1[512 * a : 512 * (a + 1), :].rearrange("(p j) r -> p j r", j=PACK))
+            w1_raw.append(raw)
+
+        def gather_words(a, c):
+            nc.vector.tensor_copy(
+                v_w[c][:, a * CHUNK : (a + 1) * CHUNK], tab_w[a][:].bitcast(U32).indirect(offsets[:, c * CHUNK // 16 : (c + 1) * CHUNK // 16])
+            )
+
+        def deal(dst, src):
+            nc.vector.tensor_copy(
+                out=dst.rearrange("p (a t m) -> p a m t", m=P, t=PACK), in_=src.rearrange("p (a m t) -> p a m t", m=P, t=PACK)
+            )
+
+        def round_w1(a, engine_copy, ms):
+            engine_copy(
+                out=w1_bf[a][:].rearrange("p (t m j) -> p m j t", t=PACK, j=PACK)[:, ms],
+                in_=w1_raw[a][:].rearrange("p j (m t) -> p m j t", t=PACK)[:, ms],
+            )
+
+        def quantize_w1(a):
+            nc.vector.quantize_mx(out=w1_w[a][:].bitcast(FP8X4), scales=w1_s[a][:], in_=w1_bf[a][:])
+
+        nc.vector.tensor_copy(picked_s[:], tab_s[:].indirect(offsets[:]))
+
+        def place_scales(queue, a, q):
+            first = 16 * a + 4 * q
+            queue.dma_start(
+                out=v_s[32 * q : 32 * q + 4, a * S : (a + 1) * S].bitcast(I32), in_=picked_s[first : first + 4, :].bitcast(I32)
+            )
+
+        places = [(a, q) for a in range(PASSES) for q in range(QUADS)]
+        for a, q in places[:2]:
+            place_scales(nc.sync, a, q)
+        load_w1(0, "slot_tab_s")
+        for a, q in places[2:]:
+            place_scales(nc.scalar, a, q)
+        gather_words(0, 0)
+        deal(w2_w[:].bitcast(U16), w2_raw[:].bitcast(U16))
+        load_w1(1, "slot_w2")
+        gather_words(1, 0)
+        deal(w2_s[:], w2_s_raw[:])
+        v_w.append(keep.tile([P, PASSES * CHUNK], U32, name="v_w1", tag="slot_w2_s", align_bytes=64))
+        gather_words(0, 1)
+        w3_raw = keep.tile([P, PASSES * H], I32, name="w3_raw", tag="slot_tab_w0", align_bytes=64)
+        nc.sync.dma_start(
+            out=w3_raw[:].rearrange("p (a e) -> p a e", a=PASSES),
+            in_=w3_words.rearrange("a p e i -> a p (e i)").bitcast(I32).rearrange("a p e -> p a e"),
+        )
+        gather_words(1, 1)
+        w4_raw = keep.tile([P, PACK, N], F32, name="w4_raw", tag="slot_tab_w1", align_bytes=64)
+        nc.sync.dma_start(out=w4_raw[:], in_=w4.rearrange("(p j) n -> p j n", j=PACK))
+        round_w1(0, nc.scalar.copy, slice(0, P // 2))
+        round_w1(0, nc.vector.tensor_copy, slice(P // 2, P))
+        ded_sb = keep.tile([P, N // P, S], F32, name="ded_sb", tag="slot_tab_s", align_bytes=64)
+        nc.sync.dma_start(out=ded_sb[:], in_=ded.rearrange("(g p) s -> p g s", p=P))
+        round_w1(1, nc.vector.tensor_copy, slice(0, P))
+        w5_w = keep.tile([P, 2 * N], U8, name="w5_w", tag="slot_w2", align_bytes=64)
+        nc.sync.dma_start(out=w5_w[:].bitcast(I32), in_=w5_words[0].bitcast(I32))
+        quantize_w1(0)
+        deal(w3_s[:], w3_s_raw[:])
+        quantize_w1(1)
+        deal(w3_w[:], w3_raw[:])
+
+        nc.gpsimd.tensor_scalar(
+            w4_bf[:].rearrange("p (m i j) -> p m j i", i=4, j=PACK), w4_raw[:].rearrange("p j (m i) -> p m j i", i=4),
+            1.0, 0.0, ALU.mult, ALU.add,
+        )
+
+        def first_stage(acc, first, width, codes, scales):
+            c, within = divmod(first, CHUNK)
+            for a in range(PASSES):
+                nc.tensor.matmul_mx(
+                    out=acc, lhsT=codes(a), lhsT_scale=scales(a), rhs=v_w[c][:, a * CHUNK + within : a * CHUNK + within + width].bitcast(FP8X4),
+                    rhs_scale=v_s[:, a * S + first : a * S + first + width], start=(a == 0), stop=(a == PASSES - 1),
+                )
+
+        def square_b(c, b2, pair):
+            for t in (2 * pair, 2 * pair + 1):
+                b = psum.tile([P, CHUNK], F32, name="b", tag="b", bufs=4)
+                first_stage(
+                    b[:], c * CHUNK, CHUNK,
+                    lambda a: w2_w[:, 2 * (a * H + t * P) : 2 * (a * H + (t + 1) * P)].bitcast(FP4X4),
+                    lambda a: w2_s[:, a * H + t * P : a * H + (t + 1) * P],
+                )
+                nc.scalar.activation(b2[:, t - 2 * pair, :], b[:], ACT.Square)
+
+        b2 = {}
+
+        def damping(u):
+            c, within = divmod(u * UNIT, CHUNK)
+            damp = []
+            for pair in range(PAIRS):
+                if within == 0:
+                    b2[pair] = keep.tile([P, 2, CHUNK], F32, name="b2_%d" % pair)
+                    square_b(c, b2[pair], pair)
+                den2 = ring.tile([P, 2, UNIT], F32, name="den2")
+                nc.scalar.activation(den2[:], b2[pair][:, :, within : within + UNIT], ACT.Square, bias=1.0)
+                factor = keep.tile([P, 2, UNIT], F32, name="damp%d_%d" % (u, pair))
+                nc.scalar.activation(factor[:], den2[:], ACT.Abs_reciprocal_sqrt)
+                damp.append(factor)
+            return damp
+
+        def features(u, damp):
+            h = keep.tile([P, PACK, UNIT], F32, name="h%d" % u)
+            acc_a, acc_c, damped = [], [], []
+            for pair in range(PAIRS):
+                acc_a.append(psum.tile([P, 2, UNIT], F32, name="acc_a", tag="a"))
+                for e in range(2):
+                    t = 2 * pair + e
+                    first_stage(
+                        acc_a[pair][:, e, :], u * UNIT, UNIT,
+                        lambda a: w1_w[a][:, t * P : (t + 1) * P].bitcast(FP8X4),
+                        lambda a: w1_s[a][:, t * P : (t + 1) * P],
+                    )
+            for pair in range(PAIRS):
+                acc_c.append(psum.tile([P, 2, UNIT], F32, name="acc_c", tag="c"))
+                for e in range(2):
+                    t = 2 * pair + e
+                    first_stage(
+                        acc_c[pair][:, e, :], u * UNIT, UNIT,
+                        lambda a: w3_w[:, a * H + t * P : a * H + (t + 1) * P].bitcast(FP8X4),
+                        lambda a: w3_s[4 * a : P, t * P : (t + 1) * P],
+                    )
+            for pair in range(PAIRS):
+                damped.append(ring.tile([P, 2, UNIT], F32, name="damped"))
+                nc.vector.tensor_tensor(damped[pair][:], acc_a[pair][:], damp[pair][:], ALU.mult)
+            for pair in range(PAIRS):
+                nc.vector.tensor_tensor(h[:, 2 * pair : 2 * pair + 2, :], acc_c[pair][:], damped[pair][:], ALU.add)
+            nc.sync.dma_start(out=out_1_rows[:, :, u * UNIT : (u + 1) * UNIT], in_=h[:])
+            return h
+
+        def round_h(h, engine_copy):
+            h_bf = ring.tile([P, PACK * UNIT], BF16, name="h_bf", align_bytes=64)
+            engine_copy(
+                out=h_bf[:].rearrange("p (m i t) -> p m t i", i=4, t=PACK), in_=h[:].rearrange("p t (m i) -> p m t i", i=4)
+            )
+            return h_bf
+
+        def second_stage(u, h_bf):
+            cols = slice(u * UNIT, (u + 1) * UNIT)
+            nc.vector.quantize_mx(out=h_w[:, cols].bitcast(FP8X4), scales=h_s[:, cols], in_=h_bf[:])
+            nc.sync.dma_start(out=words(out_2, 0)[:, cols], in_=h_w[:, cols].bitcast(I32))
+            y2 = psum.tile([P, GROUPS, UNIT], F32, name="y2", tag="b", bufs=4)
+            y1 = psum.tile([P, GROUPS, UNIT], F32, name="y1", tag="b", bufs=4)
+            for g in range(GROUPS):
+                nc.tensor.matmul_mx(
+                    out=y2[:, g, :], lhsT=w5_w[:, 2 * g * P : 2 * (g + 1) * P].bitcast(FP4X4), lhsT_scale=w5_s[:, g * P : (g + 1) * P],
+                    rhs=h_w[:, cols].bitcast(FP8X4), rhs_scale=h_s[:, cols], start=True, stop=True,
+                )
+            for g in range(GROUPS):
+                nc.tensor.matmul_mx(
+                    out=y1[:, g, :], lhsT=w4_w[:, g * P : (g + 1) * P].bitcast(FP8X4), lhsT_scale=w4_s[:, g * P : (g + 1) * P],
+                    rhs=h_w[:, cols].bitcast(FP8X4), rhs_scale=h_s[:, cols], start=True, stop=True,
+                )
+            y2_sb = ring.tile([P, GROUPS, UNIT], F32, name="y2_sb")
+            nc.scalar.copy(y2_sb[:], y2[:])
+            return y1, y2_sb
+
+        def larger_score(y1, y2_sb):
+            larger = ring.tile([P, GROUPS, UNIT], F32, name="larger")
+            nc.vector.tensor_tensor(larger[:], y1[:], y2_sb[:], ALU.max)
+            return larger
+
+        def payout(u, larger):
+            cols = slice(u * UNIT, (u + 1) * UNIT)
+            score = keep.tile([P, GROUPS, UNIT], F32, name="score%d" % u)
+            nc.vector.tensor_tensor(score[:], larger[:], ded_sb[:, :, cols], ALU.subtract)
+            nc.sync.dma_start(out=out_0_rows[:, :, cols], in_=score[:])
+
+        damps = [damping(0), damping(1), damping(2)]
+        scores = None
+        for u in range(UNITS):
+            h = features(u, damps[u])
+            h_bf = round_h(h, nc.vector.tensor_copy if u < 2 else nc.scalar.copy)
+            if u == 0:
+                nc.vector.quantize_mx(out=w4_w[:].bitcast(FP8X4), scales=w4_s[:], in_=w4_bf[:])
+            else:
+                larger = larger_score(*scores)
+            scores = second_stage(u, h_bf)
+            if u > 0:
+                payout(u - 1, larger)
+            else:
+                damps.append(damping(UNITS - 1))
+        for q in range(QUADS):
+            nc.sync.dma_start(out=out_3[0, 4 * q : 4 * q + 4, :].bitcast(I32), in_=h_s[32 * q : 32 * q + 4, :].bitcast(I32))
+        payout(UNITS - 1, larger_score(*scores))

@@ -35,24 +35,23 @@ def tile_list_crop_index_payout_kernel(
     nc = tc.nc
     with ExitStack() as ctx:
         keep = ctx.enter_context(tc.tile_pool(name="keep", bufs=1))
+        shared = ctx.enter_context(tc.tile_pool(name="shared", bufs=1))
         ring = ctx.enter_context(tc.tile_pool(name="ring", bufs=2))
         psum = ctx.enter_context(tc.psum_pool(name="psum", bufs=2))
 
         offsets = keep.tile([P, S // 16], U16, name="offsets")
         tab_w = [keep.tile([P, T], I32, name="tab_w%d" % a, tag="slot_tab_w%d" % a, align_bytes=64) for a in range(PASSES)]
         tab_s = keep.tile([P, T], U8, name="tab_s", tag="slot_tab_s", align_bytes=64)
-        v_w = [keep.tile([P, PASSES * CHUNK], U32, name="v_w0", align_bytes=64)]
+        v_w = [[keep.tile([P, CHUNK], U32, name="v_w%d_%d" % (a, c), align_bytes=64) for c in range(CHUNKS)] for a in range(PASSES)]
         picked_s = keep.tile([P, S], U8, name="picked_s", align_bytes=64)
         v_s = keep.tile([P, PASSES * S], U8, name="v_s", align_bytes=64)
         w1_bf = [keep.tile([P, PACK * H], BF16, name="w1_bf%d" % a, align_bytes=64) for a in range(PASSES)]
         w1_w = [keep.tile([P, H], U32, name="w1_w%d" % a, align_bytes=64) for a in range(PASSES)]
         w1_s = [keep.tile([P, H], U8, name="w1_s%d" % a, align_bytes=64) for a in range(PASSES)]
-        w2_raw = keep.tile([P, PASSES * 2 * H], U8, name="w2_raw", tag="slot_w2", align_bytes=64)
+        w2_raw = shared.tile([P, PASSES * 2 * H], U8, name="w2_raw", offset=8192 - 64, align_bytes=64)
         w2_w = keep.tile([P, PASSES * 2 * H], U8, name="w2_w", align_bytes=64)
         w3_w = keep.tile([P, PASSES * H], I32, name="w3_w", align_bytes=64)
-        w2_s_raw = keep.tile([P, PASSES * H], U8, name="w2_s_raw", tag="slot_w2_s", align_bytes=64)
-        w3_s_raw = keep.tile([P, H], U8, name="w3_s_raw", align_bytes=64)
-        w5_s = keep.tile([P, N], U8, name="w5_s", align_bytes=64)
+        landing = keep.tile([P, PASSES * H], U8, name="landing", align_bytes=64)
         w2_s = keep.tile([P, PASSES * H], U8, name="w2_s", align_bytes=64)
         w3_s = keep.tile([P, H], U8, name="w3_s", align_bytes=64)
         w4_bf = keep.tile([P, PACK * N], BF16, name="w4_bf", align_bytes=64)
@@ -65,15 +64,10 @@ def tile_list_crop_index_payout_kernel(
         warm = keep.tile([P, 1], F32, name="warm")
         warm_out = keep.tile([P, 1], F32, name="warm_out")
 
-        for plane in (w2_s_raw[:], tab_s[32:64, :], tab_s[64:P, :]):
+        for plane in (landing[:], tab_s[32:64, :], tab_s[64:P, :]):
             nc.vector.memset(plane.bitcast(I32), 0)
         nc.vector.memset(warm[:], 1.0)
-        for plane in (v_s, w3_s_raw, w5_s):
-            nc.gpsimd.memset(plane[:].bitcast(I32), 0)
-        for q in range(QUADS):
-            nc.gpsimd.dma_start(out=w3_s_raw[32 * q : 32 * q + 8, :].bitcast(I32), in_=w3_scales[:, 4 * q : 4 * q + 4, :].bitcast(I32))
-        for q in range(QUADS):
-            nc.gpsimd.dma_start(out=w5_s[32 * q : 32 * q + 4, :].bitcast(I32), in_=w5_scales[0, 4 * q : 4 * q + 4, :].bitcast(I32))
+        nc.gpsimd.memset(v_s[:].bitcast(I32), 0)
 
         def words(dram, a):
             return dram[a].rearrange("p e i -> p (e i)").bitcast(I32)
@@ -87,20 +81,19 @@ def tile_list_crop_index_payout_kernel(
         nc.sync.dma_start(out=tab_w[1][:], in_=words(tab_words, 1))
         for q in range(QUADS):
             nc.scalar.dma_start(
-                out=w2_s_raw[32 * q : 32 * q + 4, :].bitcast(I32).rearrange("r (a e) -> r a e", a=PASSES),
+                out=landing[32 * q : 32 * q + 4, :].bitcast(I32).rearrange("r (a e) -> r a e", a=PASSES),
                 in_=w2_scales.bitcast(I32)[:, 4 * q : 4 * q + 4, :].rearrange("a r e -> r a e"),
             )
         nc.scalar.activation(warm_out[:], warm[:], ACT.Abs_reciprocal_sqrt)
         w1_raw = []
 
-        def load_w1(a, slot):
-            raw = keep.tile([P, PACK, H], F32, name="w1_raw%d" % a, tag=slot, align_bytes=64)
-            nc.sync.dma_start(out=raw[:], in_=w1[512 * a : 512 * (a + 1), :].rearrange("(p j) r -> p j r", j=PACK))
+        def load_w1(a, queue, raw):
+            queue.dma_start(out=raw[:], in_=w1[512 * a : 512 * (a + 1), :].rearrange("(p j) r -> p j r", j=PACK))
             w1_raw.append(raw)
 
         def gather_words(a, c):
             nc.vector.tensor_copy(
-                v_w[c][:, a * CHUNK : (a + 1) * CHUNK], tab_w[a][:].bitcast(U32).indirect(offsets[:, c * CHUNK // 16 : (c + 1) * CHUNK // 16])
+                v_w[a][c][:], tab_w[a][:].bitcast(U32).indirect(offsets[:, c * CHUNK // 16 : (c + 1) * CHUNK // 16])
             )
 
         def deal(dst, src):
@@ -127,22 +120,25 @@ def tile_list_crop_index_payout_kernel(
 
         places = [(a, q) for a in range(PASSES) for q in range(QUADS)]
         for a, q in places[:2]:
-            place_scales(nc.sync, a, q)
-        load_w1(0, "slot_tab_s")
-        for a, q in places[2:]:
             place_scales(nc.scalar, a, q)
+        load_w1(0, nc.scalar, keep.tile([P, PACK, H], F32, name="w1_raw0", tag="slot_tab_s", align_bytes=64))
+        for a, q in places[2:]:
+            place_scales(nc.sync, a, q)
         gather_words(0, 0)
-        deal(w2_w[:].bitcast(U16), w2_raw[:].bitcast(U16))
-        load_w1(1, "slot_w2")
-        gather_words(1, 0)
-        deal(w2_s[:], w2_s_raw[:])
-        v_w.append(keep.tile([P, PASSES * CHUNK], U32, name="v_w1", tag="slot_w2_s", align_bytes=64))
         gather_words(0, 1)
-        w3_raw = keep.tile([P, PASSES * H], I32, name="w3_raw", tag="slot_tab_w0", align_bytes=64)
+        deal(w2_w[:].bitcast(U16), w2_raw[:].bitcast(U16))
+        load_w1(1, nc.sync, shared.tile([P, PACK, H], F32, name="w1_raw1", offset=0, align_bytes=64))
+        w3_raw = shared.tile([P, PASSES * H], I32, name="w3_raw", offset=9216, align_bytes=64)
         nc.sync.dma_start(
             out=w3_raw[:].rearrange("p (a e) -> p a e", a=PASSES),
             in_=w3_words.rearrange("a p e i -> a p (e i)").bitcast(I32).rearrange("a p e -> p a e"),
         )
+        w5_w = shared.tile([P, 2 * N], U8, name="w5_w", offset=8192, align_bytes=64)
+        nc.sync.dma_start(out=w5_w[:].bitcast(I32), in_=w5_words[0].bitcast(I32))
+        gather_words(1, 0)
+        deal(w2_s[:], landing[:])
+        for q in range(QUADS):
+            nc.sync.dma_start(out=landing[32 * q : 32 * q + 8, 0:H].bitcast(I32), in_=w3_scales[:, 4 * q : 4 * q + 4, :].bitcast(I32))
         gather_words(1, 1)
         w4_raw = keep.tile([P, PACK, N], F32, name="w4_raw", tag="slot_tab_w1", align_bytes=64)
         nc.sync.dma_start(out=w4_raw[:], in_=w4.rearrange("(p j) n -> p j n", j=PACK))
@@ -151,13 +147,13 @@ def tile_list_crop_index_payout_kernel(
         ded_sb = keep.tile([P, N // P, S], F32, name="ded_sb", tag="slot_tab_s", align_bytes=64)
         nc.sync.dma_start(out=ded_sb[:], in_=ded.rearrange("(g p) s -> p g s", p=P))
         round_w1(1, nc.vector.tensor_copy, slice(0, P))
-        w5_w = keep.tile([P, 2 * N], U8, name="w5_w", tag="slot_w2", align_bytes=64)
-        nc.sync.dma_start(out=w5_w[:].bitcast(I32), in_=w5_words[0].bitcast(I32))
         quantize_w1(0)
-        deal(w3_s[:], w3_s_raw[:])
-        quantize_w1(1)
         deal(w3_w[:], w3_raw[:])
-
+        quantize_w1(1)
+        deal(w3_s[:], landing[:, 0:H])
+        w5_s = landing
+        for q in range(QUADS):
+            nc.sync.dma_start(out=w5_s[32 * q : 32 * q + 4, 0:N].bitcast(I32), in_=w5_scales[0, 4 * q : 4 * q + 4, :].bitcast(I32))
         nc.gpsimd.tensor_scalar(
             w4_bf[:].rearrange("p (m i j) -> p m j i", i=4, j=PACK), w4_raw[:].rearrange("p j (m i) -> p m j i", i=4),
             1.0, 0.0, ALU.mult, ALU.add,
@@ -167,31 +163,28 @@ def tile_list_crop_index_payout_kernel(
             c, within = divmod(first, CHUNK)
             for a in range(PASSES):
                 nc.tensor.matmul_mx(
-                    out=acc, lhsT=codes(a), lhsT_scale=scales(a), rhs=v_w[c][:, a * CHUNK + within : a * CHUNK + within + width].bitcast(FP8X4),
+                    out=acc, lhsT=codes(a), lhsT_scale=scales(a), rhs=v_w[a][c][:, within : within + width].bitcast(FP8X4),
                     rhs_scale=v_s[:, a * S + first : a * S + first + width], start=(a == 0), stop=(a == PASSES - 1),
                 )
 
-        def square_b(c, b2, pair):
-            for t in (2 * pair, 2 * pair + 1):
+        def square_b(c):
+            b2 = keep.tile([P, PACK, CHUNK], F32, name="b2")
+            for t in range(PACK):
                 b = psum.tile([P, CHUNK], F32, name="b", tag="b", bufs=4)
                 first_stage(
                     b[:], c * CHUNK, CHUNK,
                     lambda a: w2_w[:, 2 * (a * H + t * P) : 2 * (a * H + (t + 1) * P)].bitcast(FP4X4),
                     lambda a: w2_s[:, a * H + t * P : a * H + (t + 1) * P],
                 )
-                nc.scalar.activation(b2[:, t - 2 * pair, :], b[:], ACT.Square)
+                nc.scalar.activation(b2[:, t, :], b[:], ACT.Square)
+            return b2
 
-        b2 = {}
-
-        def damping(u):
-            c, within = divmod(u * UNIT, CHUNK)
+        def damping(u, b2):
+            within = u * UNIT % CHUNK
             damp = []
             for pair in range(PAIRS):
-                if within == 0:
-                    b2[pair] = keep.tile([P, 2, CHUNK], F32, name="b2_%d" % pair)
-                    square_b(c, b2[pair], pair)
                 den2 = ring.tile([P, 2, UNIT], F32, name="den2")
-                nc.scalar.activation(den2[:], b2[pair][:, :, within : within + UNIT], ACT.Square, bias=1.0)
+                nc.scalar.activation(den2[:], b2[:, 2 * pair : 2 * pair + 2, within : within + UNIT], ACT.Square, bias=1.0)
                 factor = keep.tile([P, 2, UNIT], F32, name="damp%d_%d" % (u, pair))
                 nc.scalar.activation(factor[:], den2[:], ACT.Abs_reciprocal_sqrt)
                 damp.append(factor)
@@ -264,7 +257,9 @@ def tile_list_crop_index_payout_kernel(
             nc.vector.tensor_tensor(score[:], larger[:], ded_sb[:, :, cols], ALU.subtract)
             nc.sync.dma_start(out=out_0_rows[:, :, cols], in_=score[:])
 
-        damps = [damping(0), damping(1), damping(2)]
+        b2 = square_b(0)
+        damps = [damping(0, b2), damping(1, b2)]
+        b2 = square_b(1)
         scores = None
         for u in range(UNITS):
             h = features(u, damps[u])
@@ -276,8 +271,8 @@ def tile_list_crop_index_payout_kernel(
             scores = second_stage(u, h_bf)
             if u > 0:
                 payout(u - 1, larger)
-            else:
-                damps.append(damping(UNITS - 1))
+            if u + 2 < UNITS:
+                damps.append(damping(u + 2, b2))
         for q in range(QUADS):
             nc.sync.dma_start(out=out_3[0, 4 * q : 4 * q + 4, :].bitcast(I32), in_=h_s[32 * q : 32 * q + 4, :].bitcast(I32))
         payout(UNITS - 1, larger_score(*scores))

@@ -52,8 +52,7 @@ def tile_list_crop_index_payout_kernel(
         w2_w = keep.tile([P, PASSES * 2 * H], U8, name="w2_w", align_bytes=64)
         w3_w = keep.tile([P, PASSES * H], I32, name="w3_w", align_bytes=64)
         landing = keep.tile([P, PASSES * H], U8, name="landing", align_bytes=64)
-        w2_s = keep.tile([P, PASSES * H], U8, name="w2_s", align_bytes=64)
-        w3_s = keep.tile([P, H], U8, name="w3_s", align_bytes=64)
+        w23_s = keep.tile([P, PASSES * H], U8, name="w23_s", align_bytes=64)
         w4_bf = keep.tile([P, PACK * N], BF16, name="w4_bf", align_bytes=64)
         w4_w = keep.tile([P, N], U32, name="w4_w", align_bytes=64)
         w4_s = keep.tile([P, N], U8, name="w4_s", align_bytes=64)
@@ -79,11 +78,13 @@ def tile_list_crop_index_payout_kernel(
             out=w2_raw[:].bitcast(I32).rearrange("p (a e) -> p a e", a=PASSES), in_=w2_words.bitcast(I32).rearrange("a p e -> p a e")
         )
         nc.sync.dma_start(out=tab_w[1][:], in_=words(tab_words, 1))
-        for q in range(QUADS):
-            nc.scalar.dma_start(
-                out=landing[32 * q : 32 * q + 4, :].bitcast(I32).rearrange("r (a e) -> r a e", a=PASSES),
-                in_=w2_scales.bitcast(I32)[:, 4 * q : 4 * q + 4, :].rearrange("a r e -> r a e"),
-            )
+        for place, scales in enumerate((w2_scales, w3_scales)):
+            for q in range(QUADS):
+                first = 32 * q + 4 * place
+                nc.scalar.dma_start(
+                    out=landing[first : first + 4, :].bitcast(I32).rearrange("r (a e) -> r a e", a=PASSES),
+                    in_=scales.bitcast(I32)[:, 4 * q : 4 * q + 4, :].rearrange("a r e -> r a e"),
+                )
         nc.scalar.activation(warm_out[:], warm[:], ACT.Abs_reciprocal_sqrt)
         w1_raw = []
 
@@ -136,28 +137,21 @@ def tile_list_crop_index_payout_kernel(
         w5_w = shared.tile([P, 2 * N], U8, name="w5_w", offset=8192, align_bytes=64)
         nc.sync.dma_start(out=w5_w[:].bitcast(I32), in_=w5_words[0].bitcast(I32))
         gather_words(1, 0)
-        deal(w2_s[:], landing[:])
-        for q in range(QUADS):
-            nc.sync.dma_start(out=landing[32 * q : 32 * q + 8, 0:H].bitcast(I32), in_=w3_scales[:, 4 * q : 4 * q + 4, :].bitcast(I32))
+        deal(w23_s[:], landing[:])
         gather_words(1, 1)
         w4_raw = keep.tile([P, PACK, N], F32, name="w4_raw", tag="slot_tab_w1", align_bytes=64)
         nc.sync.dma_start(out=w4_raw[:], in_=w4.rearrange("(p j) n -> p j n", j=PACK))
+        w5_s = landing
+        for q in range(QUADS):
+            nc.sync.dma_start(out=w5_s[32 * q : 32 * q + 4, 0:N].bitcast(I32), in_=w5_scales[0, 4 * q : 4 * q + 4, :].bitcast(I32))
         round_w1(0, nc.scalar.copy, slice(0, P // 2))
         round_w1(0, nc.vector.tensor_copy, slice(P // 2, P))
         ded_sb = keep.tile([P, N // P, S], F32, name="ded_sb", tag="slot_tab_s", align_bytes=64)
         nc.sync.dma_start(out=ded_sb[:], in_=ded.rearrange("(g p) s -> p g s", p=P))
-        round_w1(1, nc.vector.tensor_copy, slice(0, P))
         quantize_w1(0)
-        deal(w3_w[:], w3_raw[:])
+        round_w1(1, nc.vector.tensor_copy, slice(0, P))
         quantize_w1(1)
-        deal(w3_s[:], landing[:, 0:H])
-        w5_s = landing
-        for q in range(QUADS):
-            nc.sync.dma_start(out=w5_s[32 * q : 32 * q + 4, 0:N].bitcast(I32), in_=w5_scales[0, 4 * q : 4 * q + 4, :].bitcast(I32))
-        nc.gpsimd.tensor_scalar(
-            w4_bf[:].rearrange("p (m i j) -> p m j i", i=4, j=PACK), w4_raw[:].rearrange("p j (m i) -> p m j i", i=4),
-            1.0, 0.0, ALU.mult, ALU.add,
-        )
+        deal(w3_w[:], w3_raw[:])
 
         def first_stage(acc, first, width, codes, scales):
             c, within = divmod(first, CHUNK)
@@ -174,7 +168,7 @@ def tile_list_crop_index_payout_kernel(
                 first_stage(
                     b[:], c * CHUNK, CHUNK,
                     lambda a: w2_w[:, 2 * (a * H + t * P) : 2 * (a * H + (t + 1) * P)].bitcast(FP4X4),
-                    lambda a: w2_s[:, a * H + t * P : a * H + (t + 1) * P],
+                    lambda a: w23_s[:, a * H + t * P : a * H + (t + 1) * P],
                 )
                 nc.scalar.activation(b2[:, t, :], b[:], ACT.Square)
             return b2
@@ -209,7 +203,7 @@ def tile_list_crop_index_payout_kernel(
                     first_stage(
                         acc_c[pair][:, e, :], u * UNIT, UNIT,
                         lambda a: w3_w[:, a * H + t * P : a * H + (t + 1) * P].bitcast(FP8X4),
-                        lambda a: w3_s[4 * a : P, t * P : (t + 1) * P],
+                        lambda a: w23_s[4:P, a * H + t * P : a * H + (t + 1) * P],
                     )
             for pair in range(PAIRS):
                 damped.append(ring.tile([P, 2, UNIT], F32, name="damped"))
@@ -263,6 +257,10 @@ def tile_list_crop_index_payout_kernel(
         scores = None
         for u in range(UNITS):
             h = features(u, damps[u])
+            if u == 0:
+                nc.vector.tensor_copy(
+                    w4_bf[:].rearrange("p (m i j) -> p m j i", i=4, j=PACK), w4_raw[:].rearrange("p j (m i) -> p m j i", i=4)
+                )
             h_bf = round_h(h, nc.vector.tensor_copy if u < 2 else nc.scalar.copy)
             if u == 0:
                 nc.vector.quantize_mx(out=w4_w[:].bitcast(FP8X4), scales=w4_s[:], in_=w4_bf[:])

@@ -40,19 +40,22 @@ def tile_list_crop_index_payout_kernel(
         psum = ctx.enter_context(tc.psum_pool(name="psum", bufs=2))
 
         offsets = keep.tile([P, S // 16], U16, name="offsets")
-        tab_w = [keep.tile([P, T], I32, name="tab_w%d" % a, tag="slot_tab_w%d" % a, align_bytes=64) for a in range(PASSES)]
-        tab_s = keep.tile([P, T], U8, name="tab_s", tag="slot_tab_s", align_bytes=64)
+        tab_w0 = keep.tile([P, T], I32, name="tab_w0", align_bytes=64)
+        tab_w1 = shared.tile([P, T], I32, name="tab_w1", offset=32768, align_bytes=64)
+        tab_w = [tab_w0, tab_w1]
+        tab_s = shared.tile([P, T], U8, name="tab_s", offset=7168, align_bytes=64)
         v_w = [[keep.tile([P, CHUNK], U32, name="v_w%d_%d" % (a, c), align_bytes=64) for c in range(CHUNKS)] for a in range(PASSES)]
         picked_s = keep.tile([P, S], U8, name="picked_s", align_bytes=64)
         v_s = keep.tile([P, PASSES * S], U8, name="v_s", align_bytes=64)
         w1_bf = [keep.tile([P, PACK * H], BF16, name="w1_bf%d" % a, align_bytes=64) for a in range(PASSES)]
         w1_w = [keep.tile([P, H], U32, name="w1_w%d" % a, align_bytes=64) for a in range(PASSES)]
         w1_s = [keep.tile([P, H], U8, name="w1_s%d" % a, align_bytes=64) for a in range(PASSES)]
-        w2_raw = shared.tile([P, PASSES * 2 * H], U8, name="w2_raw", offset=8192 - 64, align_bytes=64)
+        w2_raw = shared.tile([P, PASSES * 2 * H], U8, name="w2_raw", offset=16384, align_bytes=64)
         w2_w = keep.tile([P, PASSES * 2 * H], U8, name="w2_w", align_bytes=64)
         w3_w = keep.tile([P, PASSES * H], I32, name="w3_w", align_bytes=64)
         landing = keep.tile([P, PASSES * H], U8, name="landing", align_bytes=64)
-        w23_s = keep.tile([P, PASSES * H], U8, name="w23_s", align_bytes=64)
+        w2_s = keep.tile([P, PASSES * H], U8, name="w2_s", align_bytes=64)
+        w3_s = keep.tile([P, H], U8, name="w3_s", align_bytes=64)
         w4_bf = keep.tile([P, PACK * N], BF16, name="w4_bf", align_bytes=64)
         w4_w = keep.tile([P, N], U32, name="w4_w", align_bytes=64)
         w4_s = keep.tile([P, N], U8, name="w4_s", align_bytes=64)
@@ -63,10 +66,11 @@ def tile_list_crop_index_payout_kernel(
         warm = keep.tile([P, 1], F32, name="warm")
         warm_out = keep.tile([P, 1], F32, name="warm_out")
 
-        for plane in (landing[:], tab_s[32:64, :], tab_s[64:P, :]):
-            nc.vector.memset(plane.bitcast(I32), 0)
-        nc.vector.memset(warm[:], 1.0)
+        nc.gpsimd.memset(landing[:].bitcast(I32), 0)
         nc.gpsimd.memset(v_s[:].bitcast(I32), 0)
+        nc.vector.memset(warm[:], 1.0)
+        for plane in (tab_s[32:64, :], tab_s[64:P, :]):
+            nc.vector.memset(plane.bitcast(I32), 0)
 
         def words(dram, a):
             return dram[a].rearrange("p e i -> p (e i)").bitcast(I32)
@@ -78,13 +82,11 @@ def tile_list_crop_index_payout_kernel(
             out=w2_raw[:].bitcast(I32).rearrange("p (a e) -> p a e", a=PASSES), in_=w2_words.bitcast(I32).rearrange("a p e -> p a e")
         )
         nc.sync.dma_start(out=tab_w[1][:], in_=words(tab_words, 1))
-        for place, scales in enumerate((w2_scales, w3_scales)):
-            for q in range(QUADS):
-                first = 32 * q + 4 * place
-                nc.scalar.dma_start(
-                    out=landing[first : first + 4, :].bitcast(I32).rearrange("r (a e) -> r a e", a=PASSES),
-                    in_=scales.bitcast(I32)[:, 4 * q : 4 * q + 4, :].rearrange("a r e -> r a e"),
-                )
+        for q in range(QUADS):
+            nc.scalar.dma_start(
+                out=landing[32 * q : 32 * q + 4, :].bitcast(I32).rearrange("r (a e) -> r a e", a=PASSES),
+                in_=w2_scales.bitcast(I32)[:, 4 * q : 4 * q + 4, :].rearrange("a r e -> r a e"),
+            )
         nc.scalar.activation(warm_out[:], warm[:], ACT.Abs_reciprocal_sqrt)
         w1_raw = []
 
@@ -120,36 +122,51 @@ def tile_list_crop_index_payout_kernel(
             )
 
         places = [(a, q) for a in range(PASSES) for q in range(QUADS)]
-        for a, q in places[:2]:
-            place_scales(nc.scalar, a, q)
-        load_w1(0, nc.scalar, keep.tile([P, PACK, H], F32, name="w1_raw0", tag="slot_tab_s", align_bytes=64))
-        for a, q in places[2:]:
+        for a, q in places[:6]:
             place_scales(nc.sync, a, q)
+        load_w1(0, nc.sync, shared.tile([P, PACK, H], F32, name="w1_raw0", offset=0, align_bytes=64))
+        for a, q in places[6:]:
+            place_scales(nc.sync, a, q)
+        halves = []
+        for half in range(2):
+            raw = shared.tile([P, PACK, H // 2], F32, name="w1_half%d" % half, offset=(8192, 13312)[half], align_bytes=64)
+            nc.sync.dma_start(
+                out=raw[:], in_=w1[512:1024, half * H // 2 : (half + 1) * H // 2].rearrange("(p j) r -> p j r", j=PACK)
+            )
+            halves.append(raw)
         gather_words(0, 0)
-        gather_words(0, 1)
         deal(w2_w[:].bitcast(U16), w2_raw[:].bitcast(U16))
-        load_w1(1, nc.sync, shared.tile([P, PACK, H], F32, name="w1_raw1", offset=0, align_bytes=64))
-        w3_raw = shared.tile([P, PASSES * H], I32, name="w3_raw", offset=9216, align_bytes=64)
+        deal(w2_s[:], landing[:])
+        gather_words(1, 0)
+        gather_words(0, 1)
+        gather_words(1, 1)
+        w3_raw = shared.tile([P, PASSES * H], I32, name="w3_raw", offset=17408, align_bytes=64)
         nc.sync.dma_start(
             out=w3_raw[:].rearrange("p (a e) -> p a e", a=PASSES),
             in_=w3_words.rearrange("a p e i -> a p (e i)").bitcast(I32).rearrange("a p e -> p a e"),
         )
-        w5_w = shared.tile([P, 2 * N], U8, name="w5_w", offset=8192, align_bytes=64)
-        nc.sync.dma_start(out=w5_w[:].bitcast(I32), in_=w5_words[0].bitcast(I32))
-        gather_words(1, 0)
-        deal(w23_s[:], landing[:])
-        gather_words(1, 1)
-        w4_raw = keep.tile([P, PACK, N], F32, name="w4_raw", tag="slot_tab_w1", align_bytes=64)
-        nc.sync.dma_start(out=w4_raw[:], in_=w4.rearrange("(p j) n -> p j n", j=PACK))
-        w5_s = landing
         for q in range(QUADS):
-            nc.sync.dma_start(out=w5_s[32 * q : 32 * q + 4, 0:N].bitcast(I32), in_=w5_scales[0, 4 * q : 4 * q + 4, :].bitcast(I32))
-        round_w1(0, nc.scalar.copy, slice(0, P // 2))
-        round_w1(0, nc.vector.tensor_copy, slice(P // 2, P))
-        ded_sb = keep.tile([P, N // P, S], F32, name="ded_sb", tag="slot_tab_s", align_bytes=64)
+            nc.sync.dma_start(
+                out=landing[32 * q : 32 * q + 8, 0:H].bitcast(I32),
+                in_=w3_scales.bitcast(I32)[:, 4 * q : 4 * q + 4, :],
+            )
+        w5_s = landing[:, H : H + N]
+        for q in range(QUADS):
+            nc.sync.dma_start(out=w5_s[32 * q : 32 * q + 4, :].bitcast(I32), in_=w5_scales[0, 4 * q : 4 * q + 4, :].bitcast(I32))
+        w4_raw = shared.tile([P, PACK, N], F32, name="w4_raw", offset=32768, align_bytes=64)
+        nc.sync.dma_start(out=w4_raw[:], in_=w4.rearrange("(p j) n -> p j n", j=PACK))
+        w5_w = shared.tile([P, 2 * N], U8, name="w5_w", offset=36864, align_bytes=64)
+        nc.sync.dma_start(out=w5_w[:].bitcast(I32), in_=w5_words[0].bitcast(I32))
+        ded_sb = shared.tile([P, N // P, S], F32, name="ded_sb", offset=37376, align_bytes=64)
         nc.sync.dma_start(out=ded_sb[:], in_=ded.rearrange("(g p) s -> p g s", p=P))
+        round_w1(0, nc.vector.tensor_copy, slice(0, P))
         quantize_w1(0)
-        round_w1(1, nc.vector.tensor_copy, slice(0, P))
+        for half in range(2):
+            nc.vector.tensor_copy(
+                out=w1_bf[1][:].rearrange("p (t m j) -> p m j t", t=PACK, j=PACK)[:, half * P // 2 : (half + 1) * P // 2],
+                in_=halves[half][:].rearrange("p j (m t) -> p m j t", t=PACK),
+            )
+        deal(w3_s[:], landing[:, 0:H])
         quantize_w1(1)
         deal(w3_w[:], w3_raw[:])
 
@@ -168,109 +185,136 @@ def tile_list_crop_index_payout_kernel(
                 first_stage(
                     b[:], c * CHUNK, CHUNK,
                     lambda a: w2_w[:, 2 * (a * H + t * P) : 2 * (a * H + (t + 1) * P)].bitcast(FP4X4),
-                    lambda a: w23_s[:, a * H + t * P : a * H + (t + 1) * P],
+                    lambda a: w2_s[:, a * H + t * P : a * H + (t + 1) * P],
                 )
                 nc.scalar.activation(b2[:, t, :], b[:], ACT.Square)
             return b2
 
+        def banks(u):
+            per = CHUNK // WIDTHS[u]
+            return [range(t, t + per) for t in range(0, PACK, per)]
+
         def damping(u, b2):
-            within = u * UNIT % CHUNK
+            within, width = FIRSTS[u] % CHUNK, WIDTHS[u]
             damp = []
-            for pair in range(PAIRS):
-                den2 = ring.tile([P, 2, UNIT], F32, name="den2")
-                nc.scalar.activation(den2[:], b2[:, 2 * pair : 2 * pair + 2, within : within + UNIT], ACT.Square, bias=1.0)
-                factor = keep.tile([P, 2, UNIT], F32, name="damp%d_%d" % (u, pair))
+            for ts in banks(u):
+                den2 = ring.tile([P, len(ts), width], F32, name="den2")
+                nc.scalar.activation(den2[:], b2[:, ts.start : ts.stop, within : within + width], ACT.Square, bias=1.0)
+                factor = keep.tile([P, len(ts), width], F32, name="damp%d_%d" % (u, ts.start))
                 nc.scalar.activation(factor[:], den2[:], ACT.Abs_reciprocal_sqrt)
                 damp.append(factor)
             return damp
 
         def features(u, damp):
-            h = keep.tile([P, PACK, UNIT], F32, name="h%d" % u)
+            first, width = FIRSTS[u], WIDTHS[u]
+            h = keep.tile([P, PACK, width], F32, name="h%d" % u)
             acc_a, acc_c, damped = [], [], []
-            for pair in range(PAIRS):
-                acc_a.append(psum.tile([P, 2, UNIT], F32, name="acc_a", tag="a"))
-                for e in range(2):
-                    t = 2 * pair + e
+            for ts in banks(u):
+                acc_a.append(psum.tile([P, len(ts), width], F32, name="acc_a", tag="a"))
+                for t in ts:
                     first_stage(
-                        acc_a[pair][:, e, :], u * UNIT, UNIT,
+                        acc_a[-1][:, t - ts.start, :], first, width,
                         lambda a: w1_w[a][:, t * P : (t + 1) * P].bitcast(FP8X4),
                         lambda a: w1_s[a][:, t * P : (t + 1) * P],
                     )
-            for pair in range(PAIRS):
-                acc_c.append(psum.tile([P, 2, UNIT], F32, name="acc_c", tag="c"))
-                for e in range(2):
-                    t = 2 * pair + e
+            for ts in banks(u):
+                acc_c.append(psum.tile([P, len(ts), width], F32, name="acc_c", tag="c"))
+                for t in ts:
                     first_stage(
-                        acc_c[pair][:, e, :], u * UNIT, UNIT,
+                        acc_c[-1][:, t - ts.start, :], first, width,
                         lambda a: w3_w[:, a * H + t * P : a * H + (t + 1) * P].bitcast(FP8X4),
-                        lambda a: w23_s[4:P, a * H + t * P : a * H + (t + 1) * P],
+                        lambda a: w3_s[4 * a : P, t * P : (t + 1) * P],
                     )
-            for pair in range(PAIRS):
-                damped.append(ring.tile([P, 2, UNIT], F32, name="damped"))
-                nc.vector.tensor_tensor(damped[pair][:], acc_a[pair][:], damp[pair][:], ALU.mult)
-            for pair in range(PAIRS):
-                nc.vector.tensor_tensor(h[:, 2 * pair : 2 * pair + 2, :], acc_c[pair][:], damped[pair][:], ALU.add)
-            nc.sync.dma_start(out=out_1_rows[:, :, u * UNIT : (u + 1) * UNIT], in_=h[:])
+            for i, ts in enumerate(banks(u)):
+                damped.append(ring.tile([P, len(ts), width], F32, name="damped"))
+                nc.vector.tensor_tensor(damped[i][:], acc_a[i][:], damp[i][:], ALU.mult)
+            for i, ts in enumerate(banks(u)):
+                nc.vector.tensor_tensor(h[:, ts.start : ts.stop, :], acc_c[i][:], damped[i][:], ALU.add)
+            nc.sync.dma_start(out=out_1_rows[:, :, first : first + width], in_=h[:])
             return h
 
-        def round_h(h, engine_copy):
-            h_bf = ring.tile([P, PACK * UNIT], BF16, name="h_bf", align_bytes=64)
-            engine_copy(
-                out=h_bf[:].rearrange("p (m i t) -> p m t i", i=4, t=PACK), in_=h[:].rearrange("p t (m i) -> p m t i", i=4)
-            )
+        def gpsimd_copy(out, in_):
+            nc.gpsimd.tensor_scalar(out, in_, 1.0, 0.0, ALU.mult, ALU.add)
+
+        def round_h(u, h, copies):
+            width = WIDTHS[u]
+            h_bf = ring.tile([P, PACK * width], BF16, name="h_bf", align_bytes=64)
+            share = width // 4 // len(copies)
+            for i, engine_copy in enumerate(copies):
+                ms = slice(i * share, (i + 1) * share)
+                engine_copy(
+                    out=h_bf[:].rearrange("p (m i t) -> p m t i", i=4, t=PACK)[:, ms],
+                    in_=h[:].rearrange("p t (m i) -> p m t i", i=4)[:, ms],
+                )
             return h_bf
 
         def second_stage(u, h_bf):
-            cols = slice(u * UNIT, (u + 1) * UNIT)
+            first, width = FIRSTS[u], WIDTHS[u]
+            cols = slice(first, first + width)
             nc.vector.quantize_mx(out=h_w[:, cols].bitcast(FP8X4), scales=h_s[:, cols], in_=h_bf[:])
             nc.sync.dma_start(out=words(out_2, 0)[:, cols], in_=h_w[:, cols].bitcast(I32))
-            y2 = psum.tile([P, GROUPS, UNIT], F32, name="y2", tag="b", bufs=4)
-            y1 = psum.tile([P, GROUPS, UNIT], F32, name="y1", tag="b", bufs=4)
+            gap = psum.tile([P, GROUPS, width], F32, name="gap", tag="b", bufs=4)
+            neg = psum.tile([P, GROUPS, width], F32, name="neg", tag="b", bufs=4)
             for g in range(GROUPS):
                 nc.tensor.matmul_mx(
-                    out=y2[:, g, :], lhsT=w5_w[:, 2 * g * P : 2 * (g + 1) * P].bitcast(FP4X4), lhsT_scale=w5_s[:, g * P : (g + 1) * P],
-                    rhs=h_w[:, cols].bitcast(FP8X4), rhs_scale=h_s[:, cols], start=True, stop=True,
+                    out=gap[:, g, :], lhsT=w4_w[:, g * P : (g + 1) * P].bitcast(FP8X4), lhsT_scale=w4_s[:, g * P : (g + 1) * P],
+                    rhs=h_w[:, cols].bitcast(FP8X4), rhs_scale=h_s[:, cols], start=True, stop=False,
                 )
+                for within in range(0, width, P):
+                    part = slice(first + within, first + within + P)
+                    nc.tensor.matmul_mx(
+                        out=gap[:, g, within : within + P], lhsT=w5_w[:, 2 * g * P : 2 * (g + 1) * P].bitcast(FP4X4),
+                        lhsT_scale=w5_s[:, g * P : (g + 1) * P],
+                        rhs=h_w[:, part].bitcast(FP8X4), rhs_scale=h_s[:, part], start=False, stop=(within + P == width),
+                    )
             for g in range(GROUPS):
                 nc.tensor.matmul_mx(
-                    out=y1[:, g, :], lhsT=w4_w[:, g * P : (g + 1) * P].bitcast(FP8X4), lhsT_scale=w4_s[:, g * P : (g + 1) * P],
+                    out=neg[:, g, :], lhsT=w4_w[:, g * P : (g + 1) * P].bitcast(FP8X4), lhsT_scale=w4_s[:, g * P : (g + 1) * P],
                     rhs=h_w[:, cols].bitcast(FP8X4), rhs_scale=h_s[:, cols], start=True, stop=True,
                 )
-            y2_sb = ring.tile([P, GROUPS, UNIT], F32, name="y2_sb")
-            nc.scalar.copy(y2_sb[:], y2[:])
-            return y1, y2_sb
+            return u, gap, neg
 
-        def larger_score(y1, y2_sb):
-            larger = ring.tile([P, GROUPS, UNIT], F32, name="larger")
-            nc.vector.tensor_tensor(larger[:], y1[:], y2_sb[:], ALU.max)
-            return larger
+        def larger_score(u, gap, neg):
+            cols = slice(FIRSTS[u], FIRSTS[u] + WIDTHS[u])
+            larger = ring.tile([P, GROUPS, WIDTHS[u]], F32, name="larger")
+            nc.vector.scalar_tensor_tensor(larger[:], gap[:], 0.0, ded_sb[:, :, cols], ALU.max, ALU.subtract)
+            return u, larger, neg
 
-        def payout(u, larger):
-            cols = slice(u * UNIT, (u + 1) * UNIT)
-            score = keep.tile([P, GROUPS, UNIT], F32, name="score%d" % u)
-            nc.vector.tensor_tensor(score[:], larger[:], ded_sb[:, :, cols], ALU.subtract)
+        def payout(u, larger, neg):
+            cols = slice(FIRSTS[u], FIRSTS[u] + WIDTHS[u])
+            score = keep.tile([P, GROUPS, WIDTHS[u]], F32, name="score%d" % u)
+            nc.vector.tensor_tensor(score[:], larger[:], neg[:], ALU.subtract)
             nc.sync.dma_start(out=out_0_rows[:, :, cols], in_=score[:])
 
+        def round_w4():
+            nc.scalar.activation(
+                w4_bf[:].rearrange("p (m i j) -> p m j i", i=4, j=PACK), w4_raw[:].rearrange("p j (m i) -> p m j i", i=4),
+                ACT.Copy, scale=-1.0,
+            )
+
+        WIDTHS = [256, 256, 256, 128, 128]
+        FIRSTS = [sum(WIDTHS[:u]) for u in range(len(WIDTHS))]
+        V, A, G = nc.vector.tensor_copy, nc.scalar.copy, gpsimd_copy
+        ROUNDERS = [[V], [A], [A], [A], [V, A]]
+        probe = keep.tile([P, 8], F32, name="probe")
         b2 = square_b(0)
         damps = [damping(0, b2), damping(1, b2)]
         b2 = square_b(1)
         scores = None
-        for u in range(UNITS):
+        for u in range(len(WIDTHS)):
             h = features(u, damps[u])
             if u == 0:
-                nc.vector.tensor_copy(
-                    w4_bf[:].rearrange("p (m i j) -> p m j i", i=4, j=PACK), w4_raw[:].rearrange("p j (m i) -> p m j i", i=4)
-                )
-            h_bf = round_h(h, nc.vector.tensor_copy if u < 2 else nc.scalar.copy)
+                round_w4()
+            h_bf = round_h(u, h, ROUNDERS[u])
             if u == 0:
                 nc.vector.quantize_mx(out=w4_w[:].bitcast(FP8X4), scales=w4_s[:], in_=w4_bf[:])
             else:
                 larger = larger_score(*scores)
             scores = second_stage(u, h_bf)
             if u > 0:
-                payout(u - 1, larger)
-            if u + 2 < UNITS:
+                payout(*larger)
+            if u + 2 < len(WIDTHS):
                 damps.append(damping(u + 2, b2))
         for q in range(QUADS):
             nc.sync.dma_start(out=out_3[0, 4 * q : 4 * q + 4, :].bitcast(I32), in_=h_s[32 * q : 32 * q + 4, :].bitcast(I32))
-        payout(UNITS - 1, larger_score(*scores))
+        payout(*larger_score(*scores))

@@ -127,32 +127,24 @@ def tile_list_crop_index_payout_kernel(
         load_w1(0, nc.sync, shared.tile([P, PACK, H], F32, name="w1_raw0", offset=0, align_bytes=64))
         for a, q in places[6:]:
             place_scales(nc.sync, a, q)
-        halves = []
-        for half in range(2):
-            raw = shared.tile([P, PACK, H // 2], F32, name="w1_half%d" % half, offset=(8192, 13312)[half], align_bytes=64)
+        landing3 = shared.tile([P, H], U8, name="landing3", offset=8192, align_bytes=64)
+        nc.gpsimd.memset(landing3[:].bitcast(I32), 0)
+        for q in range(QUADS):
             nc.sync.dma_start(
-                out=raw[:], in_=w1[512:1024, half * H // 2 : (half + 1) * H // 2].rearrange("(p j) r -> p j r", j=PACK)
+                out=landing3[32 * q : 32 * q + 8, :].bitcast(I32), in_=w3_scales.bitcast(I32)[:, 4 * q : 4 * q + 4, :]
             )
-            halves.append(raw)
         gather_words(0, 0)
         deal(w2_w[:].bitcast(U16), w2_raw[:].bitcast(U16))
         deal(w2_s[:], landing[:])
         gather_words(1, 0)
         gather_words(0, 1)
         gather_words(1, 1)
+        load_w1(1, nc.sync, shared.tile([P, PACK, H], F32, name="w1_raw1", offset=9216, align_bytes=64))
         w3_raw = shared.tile([P, PASSES * H], I32, name="w3_raw", offset=17408, align_bytes=64)
         nc.sync.dma_start(
             out=w3_raw[:].rearrange("p (a e) -> p a e", a=PASSES),
             in_=w3_words.rearrange("a p e i -> a p (e i)").bitcast(I32).rearrange("a p e -> p a e"),
         )
-        for q in range(QUADS):
-            nc.sync.dma_start(
-                out=landing[32 * q : 32 * q + 8, 0:H].bitcast(I32),
-                in_=w3_scales.bitcast(I32)[:, 4 * q : 4 * q + 4, :],
-            )
-        w5_s = landing[:, H : H + N]
-        for q in range(QUADS):
-            nc.sync.dma_start(out=w5_s[32 * q : 32 * q + 4, :].bitcast(I32), in_=w5_scales[0, 4 * q : 4 * q + 4, :].bitcast(I32))
         w4_raw = shared.tile([P, PACK, N], F32, name="w4_raw", offset=32768, align_bytes=64)
         nc.sync.dma_start(out=w4_raw[:], in_=w4.rearrange("(p j) n -> p j n", j=PACK))
         w5_w = shared.tile([P, 2 * N], U8, name="w5_w", offset=36864, align_bytes=64)
@@ -161,12 +153,11 @@ def tile_list_crop_index_payout_kernel(
         nc.sync.dma_start(out=ded_sb[:], in_=ded.rearrange("(g p) s -> p g s", p=P))
         round_w1(0, nc.vector.tensor_copy, slice(0, P))
         quantize_w1(0)
-        for half in range(2):
-            nc.vector.tensor_copy(
-                out=w1_bf[1][:].rearrange("p (t m j) -> p m j t", t=PACK, j=PACK)[:, half * P // 2 : (half + 1) * P // 2],
-                in_=halves[half][:].rearrange("p j (m t) -> p m j t", t=PACK),
-            )
-        deal(w3_s[:], landing[:, 0:H])
+        deal(w3_s[:], landing3[:])
+        w5_s = landing3[:, 0:N]
+        for q in range(QUADS):
+            nc.sync.dma_start(out=w5_s[32 * q : 32 * q + 4, :].bitcast(I32), in_=w5_scales[0, 4 * q : 4 * q + 4, :].bitcast(I32))
+        round_w1(1, nc.vector.tensor_copy, slice(0, P))
         quantize_w1(1)
         deal(w3_w[:], w3_raw[:])
 
@@ -207,7 +198,7 @@ def tile_list_crop_index_payout_kernel(
 
         def features(u, damp):
             first, width = FIRSTS[u], WIDTHS[u]
-            h = keep.tile([P, PACK, width], F32, name="h%d" % u)
+            h = h_all[first // UNIT][:, :, first % UNIT : first % UNIT + width]
             acc_a, acc_c, damped = [], [], []
             for ts in banks(u):
                 acc_a.append(psum.tile([P, len(ts), width], F32, name="acc_a", tag="a"))
@@ -230,7 +221,9 @@ def tile_list_crop_index_payout_kernel(
                 nc.vector.tensor_tensor(damped[i][:], acc_a[i][:], damp[i][:], ALU.mult)
             for i, ts in enumerate(banks(u)):
                 nc.vector.tensor_tensor(h[:, ts.start : ts.stop, :], acc_c[i][:], damped[i][:], ALU.add)
-            nc.sync.dma_start(out=out_1_rows[:, :, first : first + width], in_=h[:])
+            if (first + width) % UNIT == 0:
+                block = first // UNIT
+                nc.sync.dma_start(out=out_1_rows[:, :, block * UNIT : (block + 1) * UNIT], in_=h_all[block][:])
             return h
 
         def gpsimd_copy(out, in_):
@@ -244,7 +237,7 @@ def tile_list_crop_index_payout_kernel(
                 ms = slice(i * share, (i + 1) * share)
                 engine_copy(
                     out=h_bf[:].rearrange("p (m i t) -> p m t i", i=4, t=PACK)[:, ms],
-                    in_=h[:].rearrange("p t (m i) -> p m t i", i=4)[:, ms],
+                    in_=h.rearrange("p t (m i) -> p m t i", i=4)[:, ms],
                 )
             return h_bf
 
@@ -252,7 +245,9 @@ def tile_list_crop_index_payout_kernel(
             first, width = FIRSTS[u], WIDTHS[u]
             cols = slice(first, first + width)
             nc.vector.quantize_mx(out=h_w[:, cols].bitcast(FP8X4), scales=h_s[:, cols], in_=h_bf[:])
-            nc.sync.dma_start(out=words(out_2, 0)[:, cols], in_=h_w[:, cols].bitcast(I32))
+            if (first + width) % CHUNK == 0:
+                done = slice(first + width - CHUNK, first + width)
+                nc.sync.dma_start(out=words(out_2, 0)[:, done], in_=h_w[:, done].bitcast(I32))
             gap = psum.tile([P, GROUPS, width], F32, name="gap", tag="b", bufs=4)
             neg = psum.tile([P, GROUPS, width], F32, name="neg", tag="b", bufs=4)
             for g in range(GROUPS):
@@ -287,15 +282,16 @@ def tile_list_crop_index_payout_kernel(
             nc.sync.dma_start(out=out_0_rows[:, :, cols], in_=score[:])
 
         def round_w4():
-            nc.scalar.activation(
+            nc.vector.tensor_scalar(
                 w4_bf[:].rearrange("p (m i j) -> p m j i", i=4, j=PACK), w4_raw[:].rearrange("p j (m i) -> p m j i", i=4),
-                ACT.Copy, scale=-1.0,
+                -1.0, None, ALU.mult,
             )
 
+        h_all = [keep.tile([P, PACK, UNIT], F32, name="h%d" % i) for i in range(UNITS)]
         WIDTHS = [256, 256, 256, 128, 128]
         FIRSTS = [sum(WIDTHS[:u]) for u in range(len(WIDTHS))]
         V, A, G = nc.vector.tensor_copy, nc.scalar.copy, gpsimd_copy
-        ROUNDERS = [[V], [A], [A], [A], [V, A]]
+        ROUNDERS = [[V], [V], [A], [A], [V, A]]
         probe = keep.tile([P, 8], F32, name="probe")
         b2 = square_b(0)
         damps = [damping(0, b2), damping(1, b2)]

@@ -56,7 +56,6 @@ def tile_list_crop_index_payout_kernel(
         landing = keep.tile([P, PASSES * H], U8, name="landing", align_bytes=64)
         w2_s = keep.tile([P, PASSES * H], U8, name="w2_s", align_bytes=64)
         w3_s = keep.tile([P, H], U8, name="w3_s", align_bytes=64)
-        w4_bf = keep.tile([P, PACK * N], BF16, name="w4_bf", align_bytes=64)
         w4_w = keep.tile([P, N], U32, name="w4_w", align_bytes=64)
         w4_s = keep.tile([P, N], U8, name="w4_s", align_bytes=64)
         out_1_rows = out_1.rearrange("(p t) s -> p t s", t=PACK)
@@ -161,6 +160,8 @@ def tile_list_crop_index_payout_kernel(
         quantize_w1(1)
         deal(w3_w[:], w3_raw[:])
 
+        w4_bf = shared.tile([P, PACK * N], BF16, name="w4_bf", offset=21440, align_bytes=64)
+
         def first_stage(acc, first, width, codes, scales):
             c, within = divmod(first, CHUNK)
             for a in range(PASSES):
@@ -181,6 +182,20 @@ def tile_list_crop_index_payout_kernel(
                 nc.scalar.activation(b2[:, t, :], b[:], ACT.Square)
             return b2
 
+        def square_b_block(block, b2):
+            c, first = divmod(block * UNIT, CHUNK)
+            for pair in range(PAIRS):
+                b = psum.tile([P, 2, UNIT], F32, name="b", tag="b", bufs=4)
+                for e in range(2):
+                    t = 2 * pair + e
+                    for within in range(0, UNIT, P):
+                        first_stage(
+                            b[:, e, within : within + P], block * UNIT + within, P,
+                            lambda a: w2_w[:, 2 * (a * H + t * P) : 2 * (a * H + (t + 1) * P)].bitcast(FP4X4),
+                            lambda a: w2_s[:, a * H + t * P : a * H + (t + 1) * P],
+                        )
+                nc.scalar.activation(b2[:, 2 * pair : 2 * pair + 2, first : first + UNIT], b[:], ACT.Square)
+
         def banks(u):
             per = CHUNK // WIDTHS[u]
             return [range(t, t + per) for t in range(0, PACK, per)]
@@ -190,7 +205,7 @@ def tile_list_crop_index_payout_kernel(
             damp = []
             for ts in banks(u):
                 den2 = ring.tile([P, len(ts), width], F32, name="den2")
-                nc.scalar.activation(den2[:], b2[:, ts.start : ts.stop, within : within + width], ACT.Square, bias=1.0)
+                nc.scalar.activation(den2[:], b2[:, ts.start : ts.stop, within : within + width], ACT.Square, bias=warm_out[:])
                 factor = keep.tile([P, len(ts), width], F32, name="damp%d_%d" % (u, ts.start))
                 nc.scalar.activation(factor[:], den2[:], ACT.Abs_reciprocal_sqrt)
                 damp.append(factor)
@@ -231,10 +246,16 @@ def tile_list_crop_index_payout_kernel(
 
         def round_h(u, h, copies):
             width = WIDTHS[u]
-            h_bf = ring.tile([P, PACK * width], BF16, name="h_bf", align_bytes=64)
+            if u < 2:
+                h_bf = shared.tile([P, PACK * width], BF16, name="h_bf%d" % u, offset=23424 + 1984 * u, align_bytes=64)
+            else:
+                h_bf = ring.tile([P, PACK * width], BF16, name="h_bf", align_bytes=64)
             share = width // 4 // len(copies)
             for i, engine_copy in enumerate(copies):
                 ms = slice(i * share, (i + 1) * share)
+                if engine_copy is gpsimd_copy:
+                    engine_copy(out=h_bf[:].rearrange("p (m t) -> p m t", t=PACK), in_=h.rearrange("p t m -> p m t"))
+                    continue
                 engine_copy(
                     out=h_bf[:].rearrange("p (m i t) -> p m t i", i=4, t=PACK)[:, ms],
                     in_=h.rearrange("p t (m i) -> p m t i", i=4)[:, ms],
@@ -282,34 +303,35 @@ def tile_list_crop_index_payout_kernel(
             nc.sync.dma_start(out=out_0_rows[:, :, cols], in_=score[:])
 
         def round_w4():
-            nc.vector.tensor_scalar(
-                w4_bf[:].rearrange("p (m i j) -> p m j i", i=4, j=PACK), w4_raw[:].rearrange("p j (m i) -> p m j i", i=4),
-                -1.0, None, ALU.mult,
+            nc.gpsimd.tensor_scalar(
+                w4_bf[:].rearrange("p (n j) -> p n j", j=PACK), w4_raw[:].rearrange("p j n -> p n j"), -1.0, 0.0, ALU.mult, ALU.add
             )
 
         h_all = [keep.tile([P, PACK, UNIT], F32, name="h%d" % i) for i in range(UNITS)]
         WIDTHS = [256, 256, 256, 128, 128]
         FIRSTS = [sum(WIDTHS[:u]) for u in range(len(WIDTHS))]
         V, A, G = nc.vector.tensor_copy, nc.scalar.copy, gpsimd_copy
-        ROUNDERS = [[V], [V], [A], [A], [V, A]]
+        ROUNDERS = [[G], [G], [A], [A], [V, A]]
         probe = keep.tile([P, 8], F32, name="probe")
         b2 = square_b(0)
         damps = [damping(0, b2), damping(1, b2)]
-        b2 = square_b(1)
+        b2 = keep.tile([P, PACK, CHUNK], F32, name="b2_late")
+        square_b_block(2, b2)
+        damps.append(damping(2, b2))
+        square_b_block(3, b2)
         scores = None
         for u in range(len(WIDTHS)):
             h = features(u, damps[u])
             if u == 0:
                 round_w4()
-            h_bf = round_h(u, h, ROUNDERS[u])
-            if u == 0:
                 nc.vector.quantize_mx(out=w4_w[:].bitcast(FP8X4), scales=w4_s[:], in_=w4_bf[:])
-            else:
+            h_bf = round_h(u, h, ROUNDERS[u])
+            if u > 0:
                 larger = larger_score(*scores)
             scores = second_stage(u, h_bf)
             if u > 0:
                 payout(*larger)
-            if u + 2 < len(WIDTHS):
+            if 2 < u + 2 < len(WIDTHS):
                 damps.append(damping(u + 2, b2))
         for q in range(QUADS):
             nc.sync.dma_start(out=out_3[0, 4 * q : 4 * q + 4, :].bitcast(I32), in_=h_s[32 * q : 32 * q + 4, :].bitcast(I32))

@@ -20,12 +20,34 @@ P = 128
 PACK = 4
 PASSES = K // (P * PACK)
 QUADS = 4
+LIST_ROWS = 16
+BANK = 512
 CHUNK = 512
 CHUNKS = S // CHUNK
-UNIT = 256
-UNITS = S // UNIT
+BLOCK = 256
+BLOCKS = S // BLOCK
 PAIRS = PACK // 2
 GROUPS = N // P
+
+WIDTHS = [BLOCK, BLOCK, BLOCK, BLOCK // 2, BLOCK // 2]
+FIRSTS = [sum(WIDTHS[:u]) for u in range(len(WIDTHS))]
+UNITS = len(WIDTHS)
+GPSIMD_UNITS = 3
+EARLY_MOVES = 6
+
+OVERLAP = 64
+AT_W1_RAW0 = 0
+AT_TAB_S = 7168
+AT_W3_ROWS = 8192
+AT_W1_RAW1 = 9216
+AT_W2_RAW = 16384
+AT_W3_RAW = 17408
+AT_W4_BF = AT_W3_RAW + 4096 - OVERLAP
+AT_H_BF = AT_W4_BF + 2048 - OVERLAP
+AT_TAB_W1 = 32768
+AT_W4_RAW = AT_TAB_W1
+AT_W5_W = AT_W4_RAW + 4096
+AT_DED = AT_W5_W + 512
 
 
 def tile_list_crop_index_payout_kernel(
@@ -39,21 +61,22 @@ def tile_list_crop_index_payout_kernel(
         ring = ctx.enter_context(tc.tile_pool(name="ring", bufs=2))
         psum = ctx.enter_context(tc.psum_pool(name="psum", bufs=2))
 
-        offsets = keep.tile([P, S // 16], U16, name="offsets")
-        tab_w0 = keep.tile([P, T], I32, name="tab_w0", align_bytes=64)
-        tab_w1 = shared.tile([P, T], I32, name="tab_w1", offset=32768, align_bytes=64)
-        tab_w = [tab_w0, tab_w1]
-        tab_s = shared.tile([P, T], U8, name="tab_s", offset=7168, align_bytes=64)
+        offsets = keep.tile([P, S // LIST_ROWS], U16, name="offsets")
+        tab_w = [
+            keep.tile([P, T], I32, name="tab_w0", align_bytes=64),
+            shared.tile([P, T], I32, name="tab_w1", offset=AT_TAB_W1, align_bytes=64),
+        ]
+        tab_s = shared.tile([P, T], U8, name="tab_s", offset=AT_TAB_S, align_bytes=64)
         v_w = [[keep.tile([P, CHUNK], U32, name="v_w%d_%d" % (a, c), align_bytes=64) for c in range(CHUNKS)] for a in range(PASSES)]
-        picked_s = keep.tile([P, S], U8, name="picked_s", align_bytes=64)
+        picked_rows = keep.tile([P, S], U8, name="picked_rows", align_bytes=64)
         v_s = keep.tile([P, PASSES * S], U8, name="v_s", align_bytes=64)
         w1_bf = [keep.tile([P, PACK * H], BF16, name="w1_bf%d" % a, align_bytes=64) for a in range(PASSES)]
         w1_w = [keep.tile([P, H], U32, name="w1_w%d" % a, align_bytes=64) for a in range(PASSES)]
         w1_s = [keep.tile([P, H], U8, name="w1_s%d" % a, align_bytes=64) for a in range(PASSES)]
-        w2_raw = shared.tile([P, PASSES * 2 * H], U8, name="w2_raw", offset=16384, align_bytes=64)
+        w2_raw = shared.tile([P, PASSES * 2 * H], U8, name="w2_raw", offset=AT_W2_RAW, align_bytes=64)
         w2_w = keep.tile([P, PASSES * 2 * H], U8, name="w2_w", align_bytes=64)
         w3_w = keep.tile([P, PASSES * H], I32, name="w3_w", align_bytes=64)
-        landing = keep.tile([P, PASSES * H], U8, name="landing", align_bytes=64)
+        w2_rows = keep.tile([P, PASSES * H], U8, name="w2_rows", align_bytes=64)
         w2_s = keep.tile([P, PASSES * H], U8, name="w2_s", align_bytes=64)
         w3_s = keep.tile([P, H], U8, name="w3_s", align_bytes=64)
         w4_w = keep.tile([P, N], U32, name="w4_w", align_bytes=64)
@@ -62,105 +85,92 @@ def tile_list_crop_index_payout_kernel(
         out_0_rows = out_0.rearrange("(g p) s -> p g s", p=P)
         h_w = keep.tile([P, S], U32, name="h_w", align_bytes=64)
         h_s = keep.tile([P, S], U8, name="h_s", align_bytes=64)
-        warm = keep.tile([P, 1], F32, name="warm")
-        warm_out = keep.tile([P, 1], F32, name="warm_out")
+        unity = keep.tile([P, 1], F32, name="unity")
+        bias_one = keep.tile([P, 1], F32, name="bias_one")
 
-        nc.gpsimd.memset(landing[:].bitcast(I32), 0)
+        nc.gpsimd.memset(w2_rows[:].bitcast(I32), 0)
         nc.gpsimd.memset(v_s[:].bitcast(I32), 0)
-        nc.vector.memset(warm[:], 1.0)
-        for plane in (tab_s[32:64, :], tab_s[64:P, :]):
-            nc.vector.memset(plane.bitcast(I32), 0)
+        nc.vector.memset(unity[:], 1.0)
+        for rows in (tab_s[32:64, :], tab_s[64:P, :]):
+            nc.vector.memset(rows.bitcast(I32), 0)
 
         def words(dram, a):
             return dram[a].rearrange("p e i -> p (e i)").bitcast(I32)
 
         nc.sync.dma_start(offsets[:], offs)
         nc.sync.dma_start(out=tab_s[0:32, :].bitcast(I32), in_=tab_scales.rearrange("a q t -> (a q) t").bitcast(I32))
-        nc.sync.dma_start(out=tab_w[0][:], in_=words(tab_words, 0))
         nc.sync.dma_start(
             out=w2_raw[:].bitcast(I32).rearrange("p (a e) -> p a e", a=PASSES), in_=w2_words.bitcast(I32).rearrange("a p e -> p a e")
         )
-        nc.sync.dma_start(out=tab_w[1][:], in_=words(tab_words, 1))
+        for a in range(PASSES):
+            nc.sync.dma_start(out=tab_w[a][:], in_=words(tab_words, a))
         for q in range(QUADS):
             nc.scalar.dma_start(
-                out=landing[32 * q : 32 * q + 4, :].bitcast(I32).rearrange("r (a e) -> r a e", a=PASSES),
+                out=w2_rows[32 * q : 32 * q + 4, :].bitcast(I32).rearrange("r (a e) -> r a e", a=PASSES),
                 in_=w2_scales.bitcast(I32)[:, 4 * q : 4 * q + 4, :].rearrange("a r e -> r a e"),
             )
-        nc.scalar.activation(warm_out[:], warm[:], ACT.Abs_reciprocal_sqrt)
-        w1_raw = []
+        nc.scalar.activation(bias_one[:], unity[:], ACT.Abs_reciprocal_sqrt)
 
-        def load_w1(a, queue, raw):
-            queue.dma_start(out=raw[:], in_=w1[512 * a : 512 * (a + 1), :].rearrange("(p j) r -> p j r", j=PACK))
-            w1_raw.append(raw)
-
-        def gather_words(a, c):
-            nc.vector.tensor_copy(
-                v_w[a][c][:], tab_w[a][:].bitcast(U32).indirect(offsets[:, c * CHUNK // 16 : (c + 1) * CHUNK // 16])
-            )
+        def load_w1(a, at):
+            raw = shared.tile([P, PACK, H], F32, name="w1_raw%d" % a, offset=at, align_bytes=64)
+            nc.sync.dma_start(out=raw[:], in_=w1[P * PACK * a : P * PACK * (a + 1), :].rearrange("(p j) r -> p j r", j=PACK))
+            return raw
 
         def deal(dst, src):
             nc.vector.tensor_copy(
                 out=dst.rearrange("p (a t m) -> p a m t", m=P, t=PACK), in_=src.rearrange("p (a m t) -> p a m t", m=P, t=PACK)
             )
 
-        def round_w1(a, engine_copy, ms):
-            engine_copy(
-                out=w1_bf[a][:].rearrange("p (t m j) -> p m j t", t=PACK, j=PACK)[:, ms],
-                in_=w1_raw[a][:].rearrange("p j (m t) -> p m j t", t=PACK)[:, ms],
+        def quantize_w1(a, raw):
+            nc.vector.tensor_copy(
+                out=w1_bf[a][:].rearrange("p (t m j) -> p m j t", t=PACK, j=PACK), in_=raw[:].rearrange("p j (m t) -> p m j t", t=PACK)
             )
-
-        def quantize_w1(a):
             nc.vector.quantize_mx(out=w1_w[a][:].bitcast(FP8X4), scales=w1_s[a][:], in_=w1_bf[a][:])
 
-        nc.vector.tensor_copy(picked_s[:], tab_s[:].indirect(offsets[:]))
+        nc.vector.tensor_copy(picked_rows[:], tab_s[:].indirect(offsets[:]))
 
-        def place_scales(queue, a, q):
-            first = 16 * a + 4 * q
-            queue.dma_start(
-                out=v_s[32 * q : 32 * q + 4, a * S : (a + 1) * S].bitcast(I32), in_=picked_s[first : first + 4, :].bitcast(I32)
-            )
-
-        places = [(a, q) for a in range(PASSES) for q in range(QUADS)]
-        for a, q in places[:6]:
-            place_scales(nc.sync, a, q)
-        load_w1(0, nc.sync, shared.tile([P, PACK, H], F32, name="w1_raw0", offset=0, align_bytes=64))
-        for a, q in places[6:]:
-            place_scales(nc.sync, a, q)
-        landing3 = shared.tile([P, H], U8, name="landing3", offset=8192, align_bytes=64)
-        nc.gpsimd.memset(landing3[:].bitcast(I32), 0)
-        for q in range(QUADS):
+        def move_scale_rows(a, q):
+            row = 16 * a + 4 * q
             nc.sync.dma_start(
-                out=landing3[32 * q : 32 * q + 8, :].bitcast(I32), in_=w3_scales.bitcast(I32)[:, 4 * q : 4 * q + 4, :]
+                out=v_s[32 * q : 32 * q + 4, a * S : (a + 1) * S].bitcast(I32), in_=picked_rows[row : row + 4, :].bitcast(I32)
             )
-        gather_words(0, 0)
+
+        moves = [(a, q) for a in range(PASSES) for q in range(QUADS)]
+        for a, q in moves[:EARLY_MOVES]:
+            move_scale_rows(a, q)
+        w1_raw0 = load_w1(0, AT_W1_RAW0)
+        for a, q in moves[EARLY_MOVES:]:
+            move_scale_rows(a, q)
+        w3_rows = shared.tile([P, H], U8, name="w3_rows", offset=AT_W3_ROWS, align_bytes=64)
+        nc.gpsimd.memset(w3_rows[:].bitcast(I32), 0)
+        for q in range(QUADS):
+            nc.sync.dma_start(out=w3_rows[32 * q : 32 * q + 8, :].bitcast(I32), in_=w3_scales.bitcast(I32)[:, 4 * q : 4 * q + 4, :])
         deal(w2_w[:].bitcast(U16), w2_raw[:].bitcast(U16))
-        deal(w2_s[:], landing[:])
-        gather_words(1, 0)
-        gather_words(0, 1)
-        gather_words(1, 1)
-        load_w1(1, nc.sync, shared.tile([P, PACK, H], F32, name="w1_raw1", offset=9216, align_bytes=64))
-        w3_raw = shared.tile([P, PASSES * H], I32, name="w3_raw", offset=17408, align_bytes=64)
+        deal(w2_s[:], w2_rows[:])
+        for c in range(CHUNKS):
+            for a in range(PASSES):
+                part = offsets[:, c * CHUNK // LIST_ROWS : (c + 1) * CHUNK // LIST_ROWS]
+                nc.vector.tensor_copy(v_w[a][c][:], tab_w[a][:].bitcast(U32).indirect(part))
+        w1_raw1 = load_w1(1, AT_W1_RAW1)
+        w3_raw = shared.tile([P, PASSES * H], I32, name="w3_raw", offset=AT_W3_RAW, align_bytes=64)
         nc.sync.dma_start(
             out=w3_raw[:].rearrange("p (a e) -> p a e", a=PASSES),
             in_=w3_words.rearrange("a p e i -> a p (e i)").bitcast(I32).rearrange("a p e -> p a e"),
         )
-        w4_raw = shared.tile([P, PACK, N], F32, name="w4_raw", offset=32768, align_bytes=64)
+        w4_raw = shared.tile([P, PACK, N], F32, name="w4_raw", offset=AT_W4_RAW, align_bytes=64)
         nc.sync.dma_start(out=w4_raw[:], in_=w4.rearrange("(p j) n -> p j n", j=PACK))
-        w5_w = shared.tile([P, 2 * N], U8, name="w5_w", offset=36864, align_bytes=64)
+        w5_w = shared.tile([P, 2 * N], U8, name="w5_w", offset=AT_W5_W, align_bytes=64)
         nc.sync.dma_start(out=w5_w[:].bitcast(I32), in_=w5_words[0].bitcast(I32))
-        ded_sb = shared.tile([P, N // P, S], F32, name="ded_sb", offset=37376, align_bytes=64)
+        ded_sb = shared.tile([P, GROUPS, S], F32, name="ded_sb", offset=AT_DED, align_bytes=64)
         nc.sync.dma_start(out=ded_sb[:], in_=ded.rearrange("(g p) s -> p g s", p=P))
-        round_w1(0, nc.vector.tensor_copy, slice(0, P))
-        quantize_w1(0)
-        deal(w3_s[:], landing3[:])
-        w5_s = landing3[:, 0:N]
+        quantize_w1(0, w1_raw0)
+        deal(w3_s[:], w3_rows[:])
+        w5_s = w3_rows[:, 0:N]
         for q in range(QUADS):
             nc.sync.dma_start(out=w5_s[32 * q : 32 * q + 4, :].bitcast(I32), in_=w5_scales[0, 4 * q : 4 * q + 4, :].bitcast(I32))
-        round_w1(1, nc.vector.tensor_copy, slice(0, P))
-        quantize_w1(1)
+        quantize_w1(1, w1_raw1)
         deal(w3_w[:], w3_raw[:])
-
-        w4_bf = shared.tile([P, PACK * N], BF16, name="w4_bf", offset=21440, align_bytes=64)
+        w4_bf = shared.tile([P, PACK * N], BF16, name="w4_bf", offset=AT_W4_BF, align_bytes=64)
 
         def first_stage(acc, first, width, codes, scales):
             c, within = divmod(first, CHUNK)
@@ -170,42 +180,38 @@ def tile_list_crop_index_payout_kernel(
                     rhs_scale=v_s[:, a * S + first : a * S + first + width], start=(a == 0), stop=(a == PASSES - 1),
                 )
 
-        def square_b(c):
-            b2 = keep.tile([P, PACK, CHUNK], F32, name="b2")
+        def product_b(acc, t, first, width):
+            first_stage(
+                acc, first, width,
+                lambda a: w2_w[:, 2 * (a * H + t * P) : 2 * (a * H + (t + 1) * P)].bitcast(FP4X4),
+                lambda a: w2_s[:, a * H + t * P : a * H + (t + 1) * P],
+            )
+
+        def square_b_chunk(c, b2):
             for t in range(PACK):
                 b = psum.tile([P, CHUNK], F32, name="b", tag="b", bufs=4)
-                first_stage(
-                    b[:], c * CHUNK, CHUNK,
-                    lambda a: w2_w[:, 2 * (a * H + t * P) : 2 * (a * H + (t + 1) * P)].bitcast(FP4X4),
-                    lambda a: w2_s[:, a * H + t * P : a * H + (t + 1) * P],
-                )
+                product_b(b[:], t, c * CHUNK, CHUNK)
                 nc.scalar.activation(b2[:, t, :], b[:], ACT.Square)
-            return b2
 
         def square_b_block(block, b2):
-            c, first = divmod(block * UNIT, CHUNK)
+            place = block * BLOCK % CHUNK
             for pair in range(PAIRS):
-                b = psum.tile([P, 2, UNIT], F32, name="b", tag="b", bufs=4)
+                b = psum.tile([P, 2, BLOCK], F32, name="b", tag="b", bufs=4)
                 for e in range(2):
-                    t = 2 * pair + e
-                    for within in range(0, UNIT, P):
-                        first_stage(
-                            b[:, e, within : within + P], block * UNIT + within, P,
-                            lambda a: w2_w[:, 2 * (a * H + t * P) : 2 * (a * H + (t + 1) * P)].bitcast(FP4X4),
-                            lambda a: w2_s[:, a * H + t * P : a * H + (t + 1) * P],
-                        )
-                nc.scalar.activation(b2[:, 2 * pair : 2 * pair + 2, first : first + UNIT], b[:], ACT.Square)
+                    for within in range(0, BLOCK, P):
+                        product_b(b[:, e, within : within + P], 2 * pair + e, block * BLOCK + within, P)
+                nc.scalar.activation(b2[:, 2 * pair : 2 * pair + 2, place : place + BLOCK], b[:], ACT.Square)
 
         def banks(u):
-            per = CHUNK // WIDTHS[u]
+            per = BANK // WIDTHS[u]
             return [range(t, t + per) for t in range(0, PACK, per)]
 
         def damping(u, b2):
-            within, width = FIRSTS[u] % CHUNK, WIDTHS[u]
+            place, width = FIRSTS[u] % CHUNK, WIDTHS[u]
             damp = []
             for ts in banks(u):
                 den2 = ring.tile([P, len(ts), width], F32, name="den2")
-                nc.scalar.activation(den2[:], b2[:, ts.start : ts.stop, within : within + width], ACT.Square, bias=warm_out[:])
+                nc.scalar.activation(den2[:], b2[:, ts.start : ts.stop, place : place + width], ACT.Square, bias=bias_one[:])
                 factor = keep.tile([P, len(ts), width], F32, name="damp%d_%d" % (u, ts.start))
                 nc.scalar.activation(factor[:], den2[:], ACT.Abs_reciprocal_sqrt)
                 damp.append(factor)
@@ -213,7 +219,8 @@ def tile_list_crop_index_payout_kernel(
 
         def features(u, damp):
             first, width = FIRSTS[u], WIDTHS[u]
-            h = h_all[first // UNIT][:, :, first % UNIT : first % UNIT + width]
+            block, place = divmod(first, BLOCK)
+            h = h_blocks[block][:, :, place : place + width]
             acc_a, acc_c, damped = [], [], []
             for ts in banks(u):
                 acc_a.append(psum.tile([P, len(ts), width], F32, name="acc_a", tag="a"))
@@ -236,29 +243,22 @@ def tile_list_crop_index_payout_kernel(
                 nc.vector.tensor_tensor(damped[i][:], acc_a[i][:], damp[i][:], ALU.mult)
             for i, ts in enumerate(banks(u)):
                 nc.vector.tensor_tensor(h[:, ts.start : ts.stop, :], acc_c[i][:], damped[i][:], ALU.add)
-            if (first + width) % UNIT == 0:
-                block = first // UNIT
-                nc.sync.dma_start(out=out_1_rows[:, :, block * UNIT : (block + 1) * UNIT], in_=h_all[block][:])
+            if place + width == BLOCK:
+                nc.sync.dma_start(out=out_1_rows[:, :, block * BLOCK : (block + 1) * BLOCK], in_=h_blocks[block][:])
             return h
 
-        def gpsimd_copy(out, in_):
-            nc.gpsimd.tensor_scalar(out, in_, 1.0, 0.0, ALU.mult, ALU.add)
-
-        def round_h(u, h, copies):
+        def round_h(u, h):
             width = WIDTHS[u]
-            if u < 2:
-                h_bf = shared.tile([P, PACK * width], BF16, name="h_bf%d" % u, offset=23424 + 1984 * u, align_bytes=64)
+            if u < GPSIMD_UNITS:
+                at = AT_H_BF + (2 * PACK * BLOCK - OVERLAP) * u
+                h_bf = shared.tile([P, PACK * width], BF16, name="h_bf%d" % u, offset=at, align_bytes=64)
+                nc.gpsimd.tensor_scalar(
+                    h_bf[:].rearrange("p (m t) -> p m t", t=PACK), h.rearrange("p t m -> p m t"), 1.0, 0.0, ALU.mult, ALU.add
+                )
             else:
                 h_bf = ring.tile([P, PACK * width], BF16, name="h_bf", align_bytes=64)
-            share = width // 4 // len(copies)
-            for i, engine_copy in enumerate(copies):
-                ms = slice(i * share, (i + 1) * share)
-                if engine_copy is gpsimd_copy:
-                    engine_copy(out=h_bf[:].rearrange("p (m t) -> p m t", t=PACK), in_=h.rearrange("p t m -> p m t"))
-                    continue
-                engine_copy(
-                    out=h_bf[:].rearrange("p (m i t) -> p m t i", i=4, t=PACK)[:, ms],
-                    in_=h.rearrange("p t (m i) -> p m t i", i=4)[:, ms],
+                nc.scalar.copy(
+                    out=h_bf[:].rearrange("p (m i t) -> p m t i", i=4, t=PACK), in_=h.rearrange("p t (m i) -> p m t i", i=4)
                 )
             return h_bf
 
@@ -271,11 +271,15 @@ def tile_list_crop_index_payout_kernel(
                 nc.sync.dma_start(out=words(out_2, 0)[:, done], in_=h_w[:, done].bitcast(I32))
             gap = psum.tile([P, GROUPS, width], F32, name="gap", tag="b", bufs=4)
             neg = psum.tile([P, GROUPS, width], F32, name="neg", tag="b", bufs=4)
-            for g in range(GROUPS):
+
+            def negated_w4(acc, g, stop):
                 nc.tensor.matmul_mx(
-                    out=gap[:, g, :], lhsT=w4_w[:, g * P : (g + 1) * P].bitcast(FP8X4), lhsT_scale=w4_s[:, g * P : (g + 1) * P],
-                    rhs=h_w[:, cols].bitcast(FP8X4), rhs_scale=h_s[:, cols], start=True, stop=False,
+                    out=acc, lhsT=w4_w[:, g * P : (g + 1) * P].bitcast(FP8X4), lhsT_scale=w4_s[:, g * P : (g + 1) * P],
+                    rhs=h_w[:, cols].bitcast(FP8X4), rhs_scale=h_s[:, cols], start=True, stop=stop,
                 )
+
+            for g in range(GROUPS):
+                negated_w4(gap[:, g, :], g, False)
                 for within in range(0, width, P):
                     part = slice(first + within, first + within + P)
                     nc.tensor.matmul_mx(
@@ -284,55 +288,46 @@ def tile_list_crop_index_payout_kernel(
                         rhs=h_w[:, part].bitcast(FP8X4), rhs_scale=h_s[:, part], start=False, stop=(within + P == width),
                     )
             for g in range(GROUPS):
-                nc.tensor.matmul_mx(
-                    out=neg[:, g, :], lhsT=w4_w[:, g * P : (g + 1) * P].bitcast(FP8X4), lhsT_scale=w4_s[:, g * P : (g + 1) * P],
-                    rhs=h_w[:, cols].bitcast(FP8X4), rhs_scale=h_s[:, cols], start=True, stop=True,
-                )
-            return u, gap, neg
+                negated_w4(neg[:, g, :], g, True)
+            return gap, neg
 
-        def larger_score(u, gap, neg):
-            cols = slice(FIRSTS[u], FIRSTS[u] + WIDTHS[u])
-            larger = ring.tile([P, GROUPS, WIDTHS[u]], F32, name="larger")
-            nc.vector.scalar_tensor_tensor(larger[:], gap[:], 0.0, ded_sb[:, :, cols], ALU.max, ALU.subtract)
-            return u, larger, neg
+        def excess(u, gap):
+            over = ring.tile([P, GROUPS, WIDTHS[u]], F32, name="over")
+            nc.vector.scalar_tensor_tensor(over[:], gap[:], 0.0, ded_sb[:, :, FIRSTS[u] : FIRSTS[u] + WIDTHS[u]], ALU.max, ALU.subtract)
+            return over
 
-        def payout(u, larger, neg):
-            cols = slice(FIRSTS[u], FIRSTS[u] + WIDTHS[u])
+        def payout(u, over, neg):
             score = keep.tile([P, GROUPS, WIDTHS[u]], F32, name="score%d" % u)
-            nc.vector.tensor_tensor(score[:], larger[:], neg[:], ALU.subtract)
-            nc.sync.dma_start(out=out_0_rows[:, :, cols], in_=score[:])
+            nc.vector.tensor_tensor(score[:], over[:], neg[:], ALU.subtract)
+            nc.sync.dma_start(out=out_0_rows[:, :, FIRSTS[u] : FIRSTS[u] + WIDTHS[u]], in_=score[:])
 
-        def round_w4():
-            nc.gpsimd.tensor_scalar(
-                w4_bf[:].rearrange("p (n j) -> p n j", j=PACK), w4_raw[:].rearrange("p j n -> p n j"), -1.0, 0.0, ALU.mult, ALU.add
-            )
+        h_blocks = [keep.tile([P, PACK, BLOCK], F32, name="h%d" % block) for block in range(BLOCKS)]
 
-        h_all = [keep.tile([P, PACK, UNIT], F32, name="h%d" % i) for i in range(UNITS)]
-        WIDTHS = [256, 256, 256, 128, 128]
-        FIRSTS = [sum(WIDTHS[:u]) for u in range(len(WIDTHS))]
-        V, A, G = nc.vector.tensor_copy, nc.scalar.copy, gpsimd_copy
-        ROUNDERS = [[G], [G], [A], [A], [V, A]]
-        probe = keep.tile([P, 8], F32, name="probe")
-        b2 = square_b(0)
-        damps = [damping(0, b2), damping(1, b2)]
-        b2 = keep.tile([P, PACK, CHUNK], F32, name="b2_late")
-        square_b_block(2, b2)
-        damps.append(damping(2, b2))
-        square_b_block(3, b2)
-        scores = None
-        for u in range(len(WIDTHS)):
-            h = features(u, damps[u])
-            if u == 0:
-                round_w4()
-                nc.vector.quantize_mx(out=w4_w[:].bitcast(FP8X4), scales=w4_s[:], in_=w4_bf[:])
-            h_bf = round_h(u, h, ROUNDERS[u])
-            if u > 0:
-                larger = larger_score(*scores)
-            scores = second_stage(u, h_bf)
-            if u > 0:
-                payout(*larger)
-            if 2 < u + 2 < len(WIDTHS):
-                damps.append(damping(u + 2, b2))
+        per_chunk = CHUNK // BLOCK
+        b2_early = keep.tile([P, PACK, CHUNK], F32, name="b2_early")
+        square_b_chunk(0, b2_early)
+        damps = [damping(u, b2_early) for u in range(per_chunk)]
+        b2_late = keep.tile([P, PACK, CHUNK], F32, name="b2_late")
+        for block in range(per_chunk, BLOCKS):
+            square_b_block(block, b2_late)
+            damps.extend(damping(u, b2_late) for u in range(UNITS) if FIRSTS[u] // BLOCK == block)
+
+        nc.gpsimd.tensor_scalar(
+            w4_bf[:].rearrange("p (n j) -> p n j", j=PACK), w4_raw[:].rearrange("p j n -> p n j"), -1.0, 0.0, ALU.mult, ALU.add
+        )
+        h = features(0, damps[0])
+        nc.vector.quantize_mx(out=w4_w[:].bitcast(FP8X4), scales=w4_s[:], in_=w4_bf[:])
+
+        h_bf = round_h(0, h)
+        h = features(1, damps[1])
+        gap, neg = second_stage(0, h_bf)
+        for u in range(1, UNITS):
+            h_bf = round_h(u, h)
+            if u + 1 < UNITS:
+                h = features(u + 1, damps[u + 1])
+            over, neg_before = excess(u - 1, gap), neg
+            gap, neg = second_stage(u, h_bf)
+            payout(u - 1, over, neg_before)
         for q in range(QUADS):
             nc.sync.dma_start(out=out_3[0, 4 * q : 4 * q + 4, :].bitcast(I32), in_=h_s[32 * q : 32 * q + 4, :].bitcast(I32))
-        payout(*larger_score(*scores))
+        payout(UNITS - 1, excess(UNITS - 1, gap), neg)

@@ -33,7 +33,6 @@ WIDTHS = [BLOCK, BLOCK, BLOCK, BLOCK // 2, BLOCK // 2]
 FIRSTS = [sum(WIDTHS[:u]) for u in range(len(WIDTHS))]
 UNITS = len(WIDTHS)
 GPSIMD_UNITS = 3
-EARLY_MOVES = 6
 
 OVERLAP = 64
 AT_W1_RAW0 = 0
@@ -98,7 +97,7 @@ def tile_list_crop_index_payout_kernel(
             return dram[a].rearrange("p e i -> p (e i)").bitcast(I32)
 
         nc.sync.dma_start(offsets[:], offs)
-        nc.sync.dma_start(out=tab_s[0:32, :].bitcast(I32), in_=tab_scales.rearrange("a q t -> (a q) t").bitcast(I32))
+        nc.sync.dma_start(out=tab_s[0:32, :].bitcast(I32), in_=tab_scales.bitcast(I32).rearrange("a q t -> q a t"))
         nc.sync.dma_start(
             out=w2_raw[:].bitcast(I32).rearrange("p (a e) -> p a e", a=PASSES), in_=w2_words.bitcast(I32).rearrange("a p e -> p a e")
         )
@@ -129,18 +128,12 @@ def tile_list_crop_index_payout_kernel(
 
         nc.vector.tensor_copy(picked_rows[:], tab_s[:].indirect(offsets[:]))
 
-        def move_scale_rows(a, q):
-            row = 16 * a + 4 * q
+        for q in range(QUADS):
             nc.sync.dma_start(
-                out=v_s[32 * q : 32 * q + 4, a * S : (a + 1) * S].bitcast(I32), in_=picked_rows[row : row + 4, :].bitcast(I32)
+                out=v_s[32 * q : 32 * q + 4, :].bitcast(I32).rearrange("r (a s) -> r a s", a=PASSES),
+                in_=picked_rows[8 * q : 8 * q + 8, :].bitcast(I32),
             )
-
-        moves = [(a, q) for a in range(PASSES) for q in range(QUADS)]
-        for a, q in moves[:EARLY_MOVES]:
-            move_scale_rows(a, q)
         w1_raw0 = load_w1(0, AT_W1_RAW0)
-        for a, q in moves[EARLY_MOVES:]:
-            move_scale_rows(a, q)
         w3_rows = shared.tile([P, H], U8, name="w3_rows", offset=AT_W3_ROWS, align_bytes=64)
         nc.gpsimd.memset(w3_rows[:].bitcast(I32), 0)
         for q in range(QUADS):
@@ -187,8 +180,8 @@ def tile_list_crop_index_payout_kernel(
                 lambda a: w2_s[:, a * H + t * P : a * H + (t + 1) * P],
             )
 
-        def square_b_chunk(c, b2):
-            for t in range(PACK):
+        def square_b_chunk(c, ts, b2):
+            for t in ts:
                 b = psum.tile([P, CHUNK], F32, name="b", tag="b", bufs=4)
                 product_b(b[:], t, c * CHUNK, CHUNK)
                 nc.scalar.activation(b2[:, t, :], b[:], ACT.Square)
@@ -206,16 +199,13 @@ def tile_list_crop_index_payout_kernel(
             per = BANK // WIDTHS[u]
             return [range(t, t + per) for t in range(0, PACK, per)]
 
-        def damping(u, b2):
+        def damping(u, ts, b2):
             place, width = FIRSTS[u] % CHUNK, WIDTHS[u]
-            damp = []
-            for ts in banks(u):
-                den2 = ring.tile([P, len(ts), width], F32, name="den2")
-                nc.scalar.activation(den2[:], b2[:, ts.start : ts.stop, place : place + width], ACT.Square, bias=bias_one[:])
-                factor = keep.tile([P, len(ts), width], F32, name="damp%d_%d" % (u, ts.start))
-                nc.scalar.activation(factor[:], den2[:], ACT.Abs_reciprocal_sqrt)
-                damp.append(factor)
-            return damp
+            den2 = ring.tile([P, len(ts), width], F32, name="den2")
+            nc.scalar.activation(den2[:], b2[:, ts.start : ts.stop, place : place + width], ACT.Square, bias=bias_one[:])
+            factor = keep.tile([P, len(ts), width], F32, name="damp%d_%d" % (u, ts.start))
+            nc.scalar.activation(factor[:], den2[:], ACT.Abs_reciprocal_sqrt)
+            return factor
 
         def features(u, damp):
             first, width = FIRSTS[u], WIDTHS[u]
@@ -305,12 +295,15 @@ def tile_list_crop_index_payout_kernel(
 
         per_chunk = CHUNK // BLOCK
         b2_early = keep.tile([P, PACK, CHUNK], F32, name="b2_early")
-        square_b_chunk(0, b2_early)
-        damps = [damping(u, b2_early) for u in range(per_chunk)]
+        damps = [[]]
+        for ts in banks(0):
+            square_b_chunk(0, ts, b2_early)
+            damps[0].append(damping(0, ts, b2_early))
+        damps.extend([damping(u, ts, b2_early) for ts in banks(u)] for u in range(1, per_chunk))
         b2_late = keep.tile([P, PACK, CHUNK], F32, name="b2_late")
         for block in range(per_chunk, BLOCKS):
             square_b_block(block, b2_late)
-            damps.extend(damping(u, b2_late) for u in range(UNITS) if FIRSTS[u] // BLOCK == block)
+            damps.extend([damping(u, ts, b2_late) for ts in banks(u)] for u in range(UNITS) if FIRSTS[u] // BLOCK == block)
 
         nc.gpsimd.tensor_scalar(
             w4_bf[:].rearrange("p (n j) -> p n j", j=PACK), w4_raw[:].rearrange("p j n -> p n j"), -1.0, 0.0, ALU.mult, ALU.add

@@ -39,8 +39,9 @@ AT_W1_RAW0 = 0
 AT_TAB_S = 7168
 AT_W3_ROWS = 8192
 AT_W1_RAW1 = 9216
-AT_W2_RAW = 16384
-AT_W3_RAW = 17408
+AT_W2_RAW = 16896
+AT_W2_S = 17408
+AT_W3_RAW = 18432
 AT_W4_BF = AT_W3_RAW + 4096 - OVERLAP
 AT_H_BF = AT_W4_BF + 2048 - OVERLAP
 AT_TAB_W1 = 32768
@@ -76,7 +77,7 @@ def tile_list_crop_index_payout_kernel(
         w2_w = keep.tile([P, PASSES * 2 * H], U8, name="w2_w", align_bytes=64)
         w3_w = keep.tile([P, PASSES * H], I32, name="w3_w", align_bytes=64)
         w2_rows = keep.tile([P, PASSES * H], U8, name="w2_rows", align_bytes=64)
-        w2_s = keep.tile([P, PASSES * H], U8, name="w2_s", align_bytes=64)
+        w2_s = shared.tile([P, PASSES * H], U8, name="w2_s", offset=AT_W2_S, align_bytes=64)
         w3_s = keep.tile([P, H], U8, name="w3_s", align_bytes=64)
         w4_w = keep.tile([P, N], U32, name="w4_w", align_bytes=64)
         w4_s = keep.tile([P, N], U8, name="w4_s", align_bytes=64)
@@ -139,11 +140,12 @@ def tile_list_crop_index_payout_kernel(
         for q in range(QUADS):
             nc.sync.dma_start(out=w3_rows[32 * q : 32 * q + 8, :].bitcast(I32), in_=w3_scales.bitcast(I32)[:, 4 * q : 4 * q + 4, :])
         deal(w2_w[:].bitcast(U16), w2_raw[:].bitcast(U16))
-        deal(w2_s[:], w2_rows[:])
-        for c in range(CHUNKS):
-            for a in range(PASSES):
-                part = offsets[:, c * CHUNK // LIST_ROWS : (c + 1) * CHUNK // LIST_ROWS]
-                nc.vector.tensor_copy(v_w[a][c][:], tab_w[a][:].bitcast(U32).indirect(part))
+        nc.gpsimd.tensor_copy(
+            out=w2_s[:].rearrange("p (a t m) -> p a t m", m=P, t=PACK), in_=w2_rows[:].rearrange("p (a m t) -> p a t m", m=P, t=PACK)
+        )
+        for a, c in ((0, 0), (0, 1), (1, 0), (1, 1)):
+            part = offsets[:, c * CHUNK // LIST_ROWS : (c + 1) * CHUNK // LIST_ROWS]
+            nc.vector.tensor_copy(v_w[a][c][:], tab_w[a][:].bitcast(U32).indirect(part))
         w1_raw1 = load_w1(1, AT_W1_RAW1)
         w3_raw = shared.tile([P, PASSES * H], I32, name="w3_raw", offset=AT_W3_RAW, align_bytes=64)
         nc.sync.dma_start(
@@ -165,47 +167,50 @@ def tile_list_crop_index_payout_kernel(
         deal(w3_w[:], w3_raw[:])
         w4_bf = shared.tile([P, PACK * N], BF16, name="w4_bf", offset=AT_W4_BF, align_bytes=64)
 
-        def first_stage(acc, first, width, codes, scales):
+        def first_stage(acc, first, width, codes, scales, order=(0, 1)):
             c, within = divmod(first, CHUNK)
-            for a in range(PASSES):
+            for a in order:
                 nc.tensor.matmul_mx(
                     out=acc, lhsT=codes(a), lhsT_scale=scales(a), rhs=v_w[a][c][:, within : within + width].bitcast(FP8X4),
-                    rhs_scale=v_s[:, a * S + first : a * S + first + width], start=(a == 0), stop=(a == PASSES - 1),
+                    rhs_scale=v_s[:, a * S + first : a * S + first + width], start=(a == order[0]), stop=(a == order[-1]),
                 )
 
-        def product_b(acc, t, first, width):
+        def product_b(acc, t, first, width, order=(0, 1)):
             first_stage(
                 acc, first, width,
                 lambda a: w2_w[:, 2 * (a * H + t * P) : 2 * (a * H + (t + 1) * P)].bitcast(FP4X4),
                 lambda a: w2_s[:, a * H + t * P : a * H + (t + 1) * P],
+                order,
             )
 
         def square_b_chunk(c, ts, b2):
             for t in ts:
                 b = psum.tile([P, CHUNK], F32, name="b", tag="b", bufs=4)
-                product_b(b[:], t, c * CHUNK, CHUNK)
+                product_b(b[:], t, c * CHUNK, CHUNK, (0, 1) if t == 0 else (1, 0))
                 nc.scalar.activation(b2[:, t, :], b[:], ACT.Square)
 
-        def square_b_block(block, b2):
+        def square_b_block(block, pair, b2):
             place = block * BLOCK % CHUNK
-            for pair in range(PAIRS):
-                b = psum.tile([P, 2, BLOCK], F32, name="b", tag="b", bufs=4)
-                for e in range(2):
-                    for within in range(0, BLOCK, P):
-                        product_b(b[:, e, within : within + P], 2 * pair + e, block * BLOCK + within, P)
-                nc.scalar.activation(b2[:, 2 * pair : 2 * pair + 2, place : place + BLOCK], b[:], ACT.Square)
+            b = psum.tile([P, 2, BLOCK], F32, name="b", tag="b", bufs=4)
+            for e in range(2):
+                for within in range(0, BLOCK, P):
+                    product_b(b[:, e, within : within + P], 2 * pair + e, block * BLOCK + within, P)
+            nc.scalar.activation(b2[:, 2 * pair : 2 * pair + 2, place : place + BLOCK], b[:], ACT.Square)
 
         def banks(u):
             per = BANK // WIDTHS[u]
             return [range(t, t + per) for t in range(0, PACK, per)]
 
-        def damping(u, ts, b2):
+        def denominator(u, ts, b2):
             place, width = FIRSTS[u] % CHUNK, WIDTHS[u]
-            den2 = ring.tile([P, len(ts), width], F32, name="den2")
+            den2 = ring.tile([P, len(ts), width], F32, name="den2", bufs=3)
             nc.scalar.activation(den2[:], b2[:, ts.start : ts.stop, place : place + width], ACT.Square, bias=bias_one[:])
-            factor = keep.tile([P, len(ts), width], F32, name="damp%d_%d" % (u, ts.start))
+            return den2
+
+        def damping(u, ts, den2):
+            factor = keep.tile([P, len(ts), WIDTHS[u]], F32, name="damp%d_%d" % (u, ts.start))
             nc.scalar.activation(factor[:], den2[:], ACT.Abs_reciprocal_sqrt)
-            return factor
+            damps[u].append(factor)
 
         def features(u, damp):
             first, width = FIRSTS[u], WIDTHS[u]
@@ -293,17 +298,32 @@ def tile_list_crop_index_payout_kernel(
 
         h_blocks = [keep.tile([P, PACK, BLOCK], F32, name="h%d" % block) for block in range(BLOCKS)]
 
-        per_chunk = CHUNK // BLOCK
+        damps = [[] for u in range(UNITS)]
+        low, high = banks(0)
         b2_early = keep.tile([P, PACK, CHUNK], F32, name="b2_early")
-        damps = [[]]
-        for ts in banks(0):
-            square_b_chunk(0, ts, b2_early)
-            damps[0].append(damping(0, ts, b2_early))
-        damps.extend([damping(u, ts, b2_early) for ts in banks(u)] for u in range(1, per_chunk))
         b2_late = keep.tile([P, PACK, CHUNK], F32, name="b2_late")
-        for block in range(per_chunk, BLOCKS):
-            square_b_block(block, b2_late)
-            damps.extend([damping(u, ts, b2_late) for ts in banks(u)] for u in range(UNITS) if FIRSTS[u] // BLOCK == block)
+        square_b_chunk(0, range(0, 3), b2_early)
+        den_a = denominator(0, low, b2_early)
+        square_b_chunk(0, range(3, 4), b2_early)
+        damping(0, low, den_a)
+        den_b = denominator(0, high, b2_early)
+        den_a = denominator(1, low, b2_early)
+        damping(0, high, den_b)
+        den_b = denominator(1, high, b2_early)
+        damping(1, low, den_a)
+        square_b_block(2, 0, b2_late)
+        damping(1, high, den_b)
+        square_b_block(2, 1, b2_late)
+        den_a = denominator(2, low, b2_late)
+        den_b = denominator(2, high, b2_late)
+        damping(2, low, den_a)
+        square_b_block(3, 0, b2_late)
+        damping(2, high, den_b)
+        square_b_block(3, 1, b2_late)
+        den_a = denominator(3, banks(3)[0], b2_late)
+        den_b = denominator(4, banks(4)[0], b2_late)
+        damping(3, banks(3)[0], den_a)
+        damping(4, banks(4)[0], den_b)
 
         nc.gpsimd.tensor_scalar(
             w4_bf[:].rearrange("p (n j) -> p n j", j=PACK), w4_raw[:].rearrange("p j n -> p n j"), -1.0, 0.0, ALU.mult, ALU.add

@@ -33,6 +33,7 @@ WIDTHS = [BLOCK, BLOCK, BLOCK, BLOCK // 2, BLOCK // 2]
 FIRSTS = [sum(WIDTHS[:u]) for u in range(len(WIDTHS))]
 UNITS = len(WIDTHS)
 GPSIMD_UNITS = 3
+CODE_STORES = {512: 0, 768: 512, 1024: 768}
 
 OVERLAP = 64
 AT_W1_RAW0 = 0
@@ -121,10 +122,12 @@ def tile_list_crop_index_payout_kernel(
                 out=dst.rearrange("p (a t m) -> p a m t", m=P, t=PACK), in_=src.rearrange("p (a m t) -> p a m t", m=P, t=PACK)
             )
 
-        def quantize_w1(a, raw):
+        def round_w1(a, raw):
             nc.vector.tensor_copy(
                 out=w1_bf[a][:].rearrange("p (t m j) -> p m j t", t=PACK, j=PACK), in_=raw[:].rearrange("p j (m t) -> p m j t", t=PACK)
             )
+
+        def quantize_w1(a):
             nc.vector.quantize_mx(out=w1_w[a][:].bitcast(FP8X4), scales=w1_s[a][:], in_=w1_bf[a][:])
 
         nc.vector.tensor_copy(picked_rows[:], tab_s[:].indirect(offsets[:]))
@@ -158,12 +161,14 @@ def tile_list_crop_index_payout_kernel(
         nc.sync.dma_start(out=w5_w[:].bitcast(I32), in_=w5_words[0].bitcast(I32))
         ded_sb = shared.tile([P, GROUPS, S], F32, name="ded_sb", offset=AT_DED, align_bytes=64)
         nc.sync.dma_start(out=ded_sb[:], in_=ded.rearrange("(g p) s -> p g s", p=P))
-        quantize_w1(0, w1_raw0)
+        round_w1(0, w1_raw0)
         deal(w3_s[:], w3_rows[:])
+        quantize_w1(0)
         w5_s = w3_rows[:, 0:N]
         for q in range(QUADS):
             nc.sync.dma_start(out=w5_s[32 * q : 32 * q + 4, :].bitcast(I32), in_=w5_scales[0, 4 * q : 4 * q + 4, :].bitcast(I32))
-        quantize_w1(1, w1_raw1)
+        round_w1(1, w1_raw1)
+        quantize_w1(1)
         deal(w3_w[:], w3_raw[:])
         w4_bf = shared.tile([P, PACK * N], BF16, name="w4_bf", offset=AT_W4_BF, align_bytes=64)
 
@@ -212,7 +217,7 @@ def tile_list_crop_index_payout_kernel(
             nc.scalar.activation(factor[:], den2[:], ACT.Abs_reciprocal_sqrt)
             damps[u].append(factor)
 
-        def features(u, damp):
+        def features(u, damp, between=None):
             first, width = FIRSTS[u], WIDTHS[u]
             block, place = divmod(first, BLOCK)
             h = h_blocks[block][:, :, place : place + width]
@@ -236,10 +241,11 @@ def tile_list_crop_index_payout_kernel(
             for i, ts in enumerate(banks(u)):
                 damped.append(ring.tile([P, len(ts), width], F32, name="damped"))
                 nc.vector.tensor_tensor(damped[i][:], acc_a[i][:], damp[i][:], ALU.mult)
+            if between:
+                between()
             for i, ts in enumerate(banks(u)):
                 nc.vector.tensor_tensor(h[:, ts.start : ts.stop, :], acc_c[i][:], damped[i][:], ALU.add)
-            if place + width == BLOCK:
-                nc.sync.dma_start(out=out_1_rows[:, :, block * BLOCK : (block + 1) * BLOCK], in_=h_blocks[block][:])
+            nc.sync.dma_start(out=out_1_rows[:, :, first : first + width], in_=h)
             return h
 
         def round_h(u, h):
@@ -261,8 +267,8 @@ def tile_list_crop_index_payout_kernel(
             first, width = FIRSTS[u], WIDTHS[u]
             cols = slice(first, first + width)
             nc.vector.quantize_mx(out=h_w[:, cols].bitcast(FP8X4), scales=h_s[:, cols], in_=h_bf[:])
-            if (first + width) % CHUNK == 0:
-                done = slice(first + width - CHUNK, first + width)
+            if first + width in CODE_STORES:
+                done = slice(CODE_STORES[first + width], first + width)
                 nc.sync.dma_start(out=words(out_2, 0)[:, done], in_=h_w[:, done].bitcast(I32))
             gap = psum.tile([P, GROUPS, width], F32, name="gap", tag="b", bufs=4)
             neg = psum.tile([P, GROUPS, width], F32, name="neg", tag="b", bufs=4)
@@ -286,16 +292,18 @@ def tile_list_crop_index_payout_kernel(
                 negated_w4(neg[:, g, :], g, True)
             return gap, neg
 
-        def excess(u, gap):
-            over = ring.tile([P, GROUPS, WIDTHS[u]], F32, name="over")
-            nc.vector.scalar_tensor_tensor(over[:], gap[:], 0.0, ded_sb[:, :, FIRSTS[u] : FIRSTS[u] + WIDTHS[u]], ALU.max, ALU.subtract)
-            return over
+        def excess(u, gap, groups):
+            cols = slice(FIRSTS[u], FIRSTS[u] + WIDTHS[u])
+            nc.vector.scalar_tensor_tensor(overs[u][:, groups, :], gap[:, groups, :], 0.0, ded_sb[:, groups, cols], ALU.max, ALU.subtract)
 
-        def payout(u, over, neg):
-            score = keep.tile([P, GROUPS, WIDTHS[u]], F32, name="score%d" % u)
-            nc.vector.tensor_tensor(score[:], over[:], neg[:], ALU.subtract)
-            nc.sync.dma_start(out=out_0_rows[:, :, FIRSTS[u] : FIRSTS[u] + WIDTHS[u]], in_=score[:])
+        def payout(u, neg, groups):
+            nc.vector.tensor_tensor(scores[u][:, groups, :], overs[u][:, groups, :], neg[:, groups, :], ALU.subtract)
 
+        def store_scores(u):
+            nc.sync.dma_start(out=out_0_rows[:, :, FIRSTS[u] : FIRSTS[u] + WIDTHS[u]], in_=scores[u][:])
+
+        overs = [keep.tile([P, GROUPS, WIDTHS[u]], F32, name="over%d" % u) for u in range(UNITS)]
+        scores = [keep.tile([P, GROUPS, WIDTHS[u]], F32, name="score%d" % u) for u in range(UNITS)]
         h_blocks = [keep.tile([P, PACK, BLOCK], F32, name="h%d" % block) for block in range(BLOCKS)]
 
         damps = [[] for u in range(UNITS)]
@@ -334,13 +342,21 @@ def tile_list_crop_index_payout_kernel(
         h_bf = round_h(0, h)
         h = features(1, damps[1])
         gap, neg = second_stage(0, h_bf)
+        both = slice(0, GROUPS)
         for u in range(1, UNITS):
             h_bf = round_h(u, h)
             if u + 1 < UNITS:
-                h = features(u + 1, damps[u + 1])
-            over, neg_before = excess(u - 1, gap), neg
+                h = features(u + 1, damps[u + 1], lambda: excess(u - 1, gap, both))
+            else:
+                excess(u - 1, gap, both)
+            neg_before = neg
             gap, neg = second_stage(u, h_bf)
-            payout(u - 1, over, neg_before)
+            payout(u - 1, neg_before, both)
+            store_scores(u - 1)
         for q in range(QUADS):
-            nc.sync.dma_start(out=out_3[0, 4 * q : 4 * q + 4, :].bitcast(I32), in_=h_s[32 * q : 32 * q + 4, :].bitcast(I32))
-        payout(UNITS - 1, excess(UNITS - 1, gap), neg)
+            nc.scalar.dma_start(out=out_3[0, 4 * q : 4 * q + 4, :].bitcast(I32), in_=h_s[32 * q : 32 * q + 4, :].bitcast(I32))
+        for g in range(GROUPS):
+            excess(UNITS - 1, gap, slice(g, g + 1))
+        for g in range(GROUPS):
+            payout(UNITS - 1, neg, slice(g, g + 1))
+        store_scores(UNITS - 1)

@@ -33,6 +33,7 @@ WIDTHS = [BLOCK, BLOCK, BLOCK, BLOCK // 2, BLOCK // 2]
 FIRSTS = [sum(WIDTHS[:u]) for u in range(len(WIDTHS))]
 UNITS = len(WIDTHS)
 GPSIMD_UNITS = 3
+SHARED_UNIT = 1
 CODE_STORES = {512: 0, 768: 512, 1024: 768}
 
 OVERLAP = 64
@@ -45,6 +46,7 @@ AT_W2_S = 17408
 AT_W3_RAW = 18432
 AT_W4_BF = AT_W3_RAW + 4096 - OVERLAP
 AT_H_BF = AT_W4_BF + 2048 - OVERLAP
+AT_SCORE = AT_H_BF + 3 * (2048 - OVERLAP)
 AT_TAB_W1 = 32768
 AT_W4_RAW = AT_TAB_W1
 AT_W5_W = AT_W4_RAW + 4096
@@ -122,13 +124,17 @@ def tile_list_crop_index_payout_kernel(
                 out=dst.rearrange("p (a t m) -> p a m t", m=P, t=PACK), in_=src.rearrange("p (a m t) -> p a m t", m=P, t=PACK)
             )
 
-        def round_w1(a, raw):
+        def round_w1(a, raw, ts):
             nc.vector.tensor_copy(
-                out=w1_bf[a][:].rearrange("p (t m j) -> p m j t", t=PACK, j=PACK), in_=raw[:].rearrange("p j (m t) -> p m j t", t=PACK)
+                out=w1_bf[a][:].rearrange("p (t m j) -> p m j t", t=PACK, j=PACK)[:, :, :, ts.start : ts.stop],
+                in_=raw[:].rearrange("p j (m t) -> p m j t", t=PACK)[:, :, :, ts.start : ts.stop],
             )
 
-        def quantize_w1(a):
-            nc.vector.quantize_mx(out=w1_w[a][:].bitcast(FP8X4), scales=w1_s[a][:], in_=w1_bf[a][:])
+        def quantize_w1(a, ts):
+            cols = slice(P * ts.start, P * ts.stop)
+            nc.vector.quantize_mx(
+                out=w1_w[a][:, cols].bitcast(FP8X4), scales=w1_s[a][:, cols], in_=w1_bf[a][:, PACK * cols.start : PACK * cols.stop]
+            )
 
         nc.vector.tensor_copy(picked_rows[:], tab_s[:].indirect(offsets[:]))
 
@@ -161,14 +167,16 @@ def tile_list_crop_index_payout_kernel(
         nc.sync.dma_start(out=w5_w[:].bitcast(I32), in_=w5_words[0].bitcast(I32))
         ded_sb = shared.tile([P, GROUPS, S], F32, name="ded_sb", offset=AT_DED, align_bytes=64)
         nc.sync.dma_start(out=ded_sb[:], in_=ded.rearrange("(g p) s -> p g s", p=P))
-        round_w1(0, w1_raw0)
+        round_w1(0, w1_raw0, range(PACK))
         deal(w3_s[:], w3_rows[:])
-        quantize_w1(0)
+        quantize_w1(0, range(PACK))
         w5_s = w3_rows[:, 0:N]
         for q in range(QUADS):
             nc.sync.dma_start(out=w5_s[32 * q : 32 * q + 4, :].bitcast(I32), in_=w5_scales[0, 4 * q : 4 * q + 4, :].bitcast(I32))
-        round_w1(1, w1_raw1)
-        quantize_w1(1)
+        for ts in (range(0, 2), range(2, 4)):
+            round_w1(1, w1_raw1, ts)
+        for ts in (range(0, 2), range(2, 4)):
+            quantize_w1(1, ts)
         deal(w3_w[:], w3_raw[:])
         w4_bf = shared.tile([P, PACK * N], BF16, name="w4_bf", offset=AT_W4_BF, align_bytes=64)
 
@@ -290,6 +298,10 @@ def tile_list_crop_index_payout_kernel(
                     )
             for g in range(GROUPS):
                 negated_w4(neg[:, g, :], g, True)
+            if u == SHARED_UNIT:
+                neg_sb = keep.tile([P, GROUPS, width], F32, name="neg_sb")
+                nc.scalar.copy(neg_sb[:], neg[:])
+                return gap, neg_sb
             return gap, neg
 
         def excess(u, gap, groups):
@@ -297,13 +309,15 @@ def tile_list_crop_index_payout_kernel(
             nc.vector.scalar_tensor_tensor(overs[u][:, groups, :], gap[:, groups, :], 0.0, ded_sb[:, groups, cols], ALU.max, ALU.subtract)
 
         def payout(u, neg, groups):
-            nc.vector.tensor_tensor(scores[u][:, groups, :], overs[u][:, groups, :], neg[:, groups, :], ALU.subtract)
+            engine = nc.gpsimd if u == SHARED_UNIT else nc.vector
+            engine.tensor_tensor(scores[u][:, groups, :], overs[u][:, groups, :], neg[:, groups, :], ALU.subtract)
 
         def store_scores(u):
             nc.sync.dma_start(out=out_0_rows[:, :, FIRSTS[u] : FIRSTS[u] + WIDTHS[u]], in_=scores[u][:])
 
         overs = [keep.tile([P, GROUPS, WIDTHS[u]], F32, name="over%d" % u) for u in range(UNITS)]
-        scores = [keep.tile([P, GROUPS, WIDTHS[u]], F32, name="score%d" % u) for u in range(UNITS)]
+        scores = [keep.tile([P, GROUPS, WIDTHS[u]], F32, name="score%d" % u) for u in range(UNITS) if u != SHARED_UNIT]
+        scores.insert(SHARED_UNIT, shared.tile([P, GROUPS, BLOCK], F32, name="score_shared", offset=AT_SCORE))
         h_blocks = [keep.tile([P, PACK, BLOCK], F32, name="h%d" % block) for block in range(BLOCKS)]
 
         damps = [[] for u in range(UNITS)]

@@ -47,7 +47,10 @@ AT_W3_RAW = 18432
 AT_W4_BF = AT_W3_RAW + 4096 - OVERLAP
 AT_H_BF = AT_W4_BF + 2048 - OVERLAP
 AT_SCORE = AT_H_BF + 3 * (2048 - OVERLAP)
-AT_TAB_W1 = 32768
+AT_H_BF_LATE = (AT_SCORE + 2048, AT_SCORE + 2048 + 1024 + 2048 - OVERLAP)
+AT_SCORE_2 = AT_H_BF_LATE[0] + 1024
+AT_OVER_3 = AT_H_BF_LATE[1] + 1024 - OVERLAP
+AT_TAB_W1 = 40960
 AT_W4_RAW = AT_TAB_W1
 AT_W5_W = AT_W4_RAW + 4096
 AT_DED = AT_W5_W + 512
@@ -76,11 +79,11 @@ def tile_list_crop_index_payout_kernel(
         w1_bf = [keep.tile([P, PACK * H], BF16, name="w1_bf%d" % a, align_bytes=64) for a in range(PASSES)]
         w1_w = [keep.tile([P, H], U32, name="w1_w%d" % a, align_bytes=64) for a in range(PASSES)]
         w1_s = [keep.tile([P, H], U8, name="w1_s%d" % a, align_bytes=64) for a in range(PASSES)]
-        w2_raw = shared.tile([P, PASSES * 2 * H], U8, name="w2_raw", offset=AT_W2_RAW, align_bytes=64)
+        w2_raw = [shared.tile([P, 2 * H], U8, name="w2_raw%d" % a, offset=AT_W2_RAW + 2 * H * a, align_bytes=64) for a in range(PASSES)]
         w2_w = keep.tile([P, PASSES * 2 * H], U8, name="w2_w", align_bytes=64)
         w3_w = keep.tile([P, PASSES * H], I32, name="w3_w", align_bytes=64)
         w2_rows = keep.tile([P, PASSES * H], U8, name="w2_rows", align_bytes=64)
-        w2_s = shared.tile([P, PASSES * H], U8, name="w2_s", offset=AT_W2_S, align_bytes=64)
+        w2_s = keep.tile([P, PASSES * H], U8, name="w2_s", align_bytes=64)
         w3_s = keep.tile([P, H], U8, name="w3_s", align_bytes=64)
         w4_w = keep.tile([P, N], U32, name="w4_w", align_bytes=64)
         w4_s = keep.tile([P, N], U8, name="w4_s", align_bytes=64)
@@ -102,11 +105,9 @@ def tile_list_crop_index_payout_kernel(
 
         nc.sync.dma_start(offsets[:], offs)
         nc.sync.dma_start(out=tab_s[0:32, :].bitcast(I32), in_=tab_scales.bitcast(I32).rearrange("a q t -> q a t"))
-        nc.sync.dma_start(
-            out=w2_raw[:].bitcast(I32).rearrange("p (a e) -> p a e", a=PASSES), in_=w2_words.bitcast(I32).rearrange("a p e -> p a e")
-        )
         for a in range(PASSES):
             nc.sync.dma_start(out=tab_w[a][:], in_=words(tab_words, a))
+            nc.sync.dma_start(out=w2_raw[a][:].bitcast(I32), in_=w2_words[a].bitcast(I32))
         for q in range(QUADS):
             nc.scalar.dma_start(
                 out=w2_rows[32 * q : 32 * q + 4, :].bitcast(I32).rearrange("r (a e) -> r a e", a=PASSES),
@@ -144,14 +145,17 @@ def tile_list_crop_index_payout_kernel(
                 in_=picked_rows[8 * q : 8 * q + 8, :].bitcast(I32),
             )
         w1_raw0 = load_w1(0, AT_W1_RAW0)
-        w3_rows = shared.tile([P, H], U8, name="w3_rows", offset=AT_W3_ROWS, align_bytes=64)
-        nc.gpsimd.memset(w3_rows[:].bitcast(I32), 0)
-        for q in range(QUADS):
-            nc.sync.dma_start(out=w3_rows[32 * q : 32 * q + 8, :].bitcast(I32), in_=w3_scales.bitcast(I32)[:, 4 * q : 4 * q + 4, :])
-        deal(w2_w[:].bitcast(U16), w2_raw[:].bitcast(U16))
         nc.gpsimd.tensor_copy(
             out=w2_s[:].rearrange("p (a t m) -> p a t m", m=P, t=PACK), in_=w2_rows[:].rearrange("p (a m t) -> p a t m", m=P, t=PACK)
         )
+        for a in range(PASSES):
+            nc.gpsimd.tensor_copy(
+                out=w2_w[:, 2 * H * a : 2 * H * (a + 1)].bitcast(U16).rearrange("p (t m) -> p t m", t=PACK),
+                in_=w2_raw[a][:].bitcast(U16).rearrange("p (m t) -> p t m", t=PACK),
+            )
+        w3_rows = w2_rows[:, 0:H]
+        for q in range(QUADS):
+            nc.sync.dma_start(out=w3_rows[32 * q + 4 : 32 * q + 12, :].bitcast(I32), in_=w3_scales.bitcast(I32)[:, 4 * q : 4 * q + 4, :])
         for a, c in ((0, 0), (0, 1), (1, 0), (1, 1)):
             part = offsets[:, c * CHUNK // LIST_ROWS : (c + 1) * CHUNK // LIST_ROWS]
             nc.vector.tensor_copy(v_w[a][c][:], tab_w[a][:].bitcast(U32).indirect(part))
@@ -168,7 +172,7 @@ def tile_list_crop_index_payout_kernel(
         ded_sb = shared.tile([P, GROUPS, S], F32, name="ded_sb", offset=AT_DED, align_bytes=64)
         nc.sync.dma_start(out=ded_sb[:], in_=ded.rearrange("(g p) s -> p g s", p=P))
         round_w1(0, w1_raw0, range(PACK))
-        deal(w3_s[:], w3_rows[:])
+        deal(w3_s[:], w3_rows)
         quantize_w1(0, range(PACK))
         w5_s = w3_rows[:, 0:N]
         for q in range(QUADS):
@@ -225,10 +229,8 @@ def tile_list_crop_index_payout_kernel(
             nc.scalar.activation(factor[:], den2[:], ACT.Abs_reciprocal_sqrt)
             damps[u].append(factor)
 
-        def features(u, damp, between=None):
+        def damped_products(u):
             first, width = FIRSTS[u], WIDTHS[u]
-            block, place = divmod(first, BLOCK)
-            h = h_blocks[block][:, :, place : place + width]
             acc_a, acc_c, damped = [], [], []
             for ts in banks(u):
                 acc_a.append(psum.tile([P, len(ts), width], F32, name="acc_a", tag="a"))
@@ -244,13 +246,17 @@ def tile_list_crop_index_payout_kernel(
                     first_stage(
                         acc_c[-1][:, t - ts.start, :], first, width,
                         lambda a: w3_w[:, a * H + t * P : a * H + (t + 1) * P].bitcast(FP8X4),
-                        lambda a: w3_s[4 * a : P, t * P : (t + 1) * P],
+                        lambda a: w3_s[4 * a + 4 : P, t * P : (t + 1) * P],
                     )
             for i, ts in enumerate(banks(u)):
                 damped.append(ring.tile([P, len(ts), width], F32, name="damped"))
-                nc.vector.tensor_tensor(damped[i][:], acc_a[i][:], damp[i][:], ALU.mult)
-            if between:
-                between()
+                nc.vector.tensor_tensor(damped[i][:], acc_a[i][:], damps[u][i][:], ALU.mult)
+            return damped, acc_c
+
+        def features(u, damped, acc_c):
+            first, width = FIRSTS[u], WIDTHS[u]
+            block, place = divmod(first, BLOCK)
+            h = h_blocks[block][:, :, place : place + width]
             for i, ts in enumerate(banks(u)):
                 nc.vector.tensor_tensor(h[:, ts.start : ts.stop, :], acc_c[i][:], damped[i][:], ALU.add)
             nc.sync.dma_start(out=out_1_rows[:, :, first : first + width], in_=h)
@@ -265,7 +271,7 @@ def tile_list_crop_index_payout_kernel(
                     h_bf[:].rearrange("p (m t) -> p m t", t=PACK), h.rearrange("p t m -> p m t"), 1.0, 0.0, ALU.mult, ALU.add
                 )
             else:
-                h_bf = ring.tile([P, PACK * width], BF16, name="h_bf", align_bytes=64)
+                h_bf = shared.tile([P, PACK * width], BF16, name="h_bf%d" % u, offset=AT_H_BF_LATE[u - GPSIMD_UNITS], align_bytes=64)
                 nc.scalar.copy(
                     out=h_bf[:].rearrange("p (m i t) -> p m t i", i=4, t=PACK), in_=h.rearrange("p t (m i) -> p m t i", i=4)
                 )
@@ -278,8 +284,9 @@ def tile_list_crop_index_payout_kernel(
             if first + width in CODE_STORES:
                 done = slice(CODE_STORES[first + width], first + width)
                 nc.sync.dma_start(out=words(out_2, 0)[:, done], in_=h_w[:, done].bitcast(I32))
-            gap = psum.tile([P, GROUPS, width], F32, name="gap", tag="b", bufs=4)
-            neg = psum.tile([P, GROUPS, width], F32, name="neg", tag="b", bufs=4)
+            tag, bufs = {3: ("a", 2), 4: ("c", 2)}.get(u, ("b", 4))
+            gap = psum.tile([P, GROUPS, width], F32, name="gap", tag=tag, bufs=bufs)
+            neg = psum.tile([P, GROUPS, width], F32, name="neg", tag=tag, bufs=bufs)
 
             def negated_w4(acc, g, stop):
                 nc.tensor.matmul_mx(
@@ -315,9 +322,11 @@ def tile_list_crop_index_payout_kernel(
         def store_scores(u):
             nc.sync.dma_start(out=out_0_rows[:, :, FIRSTS[u] : FIRSTS[u] + WIDTHS[u]], in_=scores[u][:])
 
-        overs = [keep.tile([P, GROUPS, WIDTHS[u]], F32, name="over%d" % u) for u in range(UNITS)]
-        scores = [keep.tile([P, GROUPS, WIDTHS[u]], F32, name="score%d" % u) for u in range(UNITS) if u != SHARED_UNIT]
+        overs = [keep.tile([P, GROUPS, WIDTHS[u]], F32, name="over%d" % u) for u in range(UNITS) if u != 3]
+        overs.insert(3, shared.tile([P, GROUPS, WIDTHS[3]], F32, name="over3", offset=AT_OVER_3))
+        scores = [keep.tile([P, GROUPS, WIDTHS[u]], F32, name="score%d" % u) for u in range(UNITS) if u not in (SHARED_UNIT, 2)]
         scores.insert(SHARED_UNIT, shared.tile([P, GROUPS, BLOCK], F32, name="score_shared", offset=AT_SCORE))
+        scores.insert(2, shared.tile([P, GROUPS, BLOCK], F32, name="score2", offset=AT_SCORE_2))
         h_blocks = [keep.tile([P, PACK, BLOCK], F32, name="h%d" % block) for block in range(BLOCKS)]
 
         damps = [[] for u in range(UNITS)]
@@ -350,27 +359,37 @@ def tile_list_crop_index_payout_kernel(
         nc.gpsimd.tensor_scalar(
             w4_bf[:].rearrange("p (n j) -> p n j", j=PACK), w4_raw[:].rearrange("p j n -> p n j"), -1.0, 0.0, ALU.mult, ALU.add
         )
-        h = features(0, damps[0])
-        nc.vector.quantize_mx(out=w4_w[:].bitcast(FP8X4), scales=w4_s[:], in_=w4_bf[:])
-
-        h_bf = round_h(0, h)
-        h = features(1, damps[1])
-        gap, neg = second_stage(0, h_bf)
         both = slice(0, GROUPS)
-        for u in range(1, UNITS):
-            h_bf = round_h(u, h)
-            if u + 1 < UNITS:
-                h = features(u + 1, damps[u + 1], lambda: excess(u - 1, gap, both))
-            else:
-                excess(u - 1, gap, both)
-            neg_before = neg
-            gap, neg = second_stage(u, h_bf)
-            payout(u - 1, neg_before, both)
-            store_scores(u - 1)
+        h = features(0, *damped_products(0))
+        nc.vector.quantize_mx(out=w4_w[:].bitcast(FP8X4), scales=w4_s[:], in_=w4_bf[:])
+        rounded = [round_h(0, h)]
+        h = features(1, *damped_products(1))
+        sums = [second_stage(0, rounded[0])]
+        rounded.append(round_h(1, h))
+        parts = damped_products(2)
+        excess(0, sums[0][0], both)
+        h = features(2, *parts)
+        sums.append(second_stage(1, rounded[1]))
+        payout(0, sums[0][1], both)
+        store_scores(0)
+        rounded.append(round_h(2, h))
+        parts = damped_products(3)
+        excess(1, sums[1][0], both)
+        rounded.append(round_h(3, features(3, *parts)))
+        parts = damped_products(4)
+        sums.append(second_stage(2, rounded[2]))
+        rounded.append(round_h(4, features(4, *parts)))
+        sums.append(second_stage(3, rounded[3]))
+        excess(2, sums[2][0], both)
+        sums.append(second_stage(4, rounded[4]))
         for q in range(QUADS):
             nc.scalar.dma_start(out=out_3[0, 4 * q : 4 * q + 4, :].bitcast(I32), in_=h_s[32 * q : 32 * q + 4, :].bitcast(I32))
-        for g in range(GROUPS):
-            excess(UNITS - 1, gap, slice(g, g + 1))
-        for g in range(GROUPS):
-            payout(UNITS - 1, neg, slice(g, g + 1))
-        store_scores(UNITS - 1)
+        payout(1, sums[1][1], both)
+        store_scores(1)
+        payout(2, sums[2][1], both)
+        store_scores(2)
+        for u in (3, 4):
+            excess(u, sums[u][0], both)
+        for u in (3, 4):
+            payout(u, sums[u][1], both)
+            store_scores(u)

@@ -149,7 +149,7 @@ def tile_list_crop_index_payout_kernel(
             out=w2_s[:].rearrange("p (a t m) -> p a t m", m=P, t=PACK), in_=w2_rows[:].rearrange("p (a m t) -> p a t m", m=P, t=PACK)
         )
         for a in range(PASSES):
-            nc.gpsimd.tensor_copy(
+            nc.scalar.copy(
                 out=w2_w[:, 2 * H * a : 2 * H * (a + 1)].bitcast(U16).rearrange("p (t m) -> p t m", t=PACK),
                 in_=w2_raw[a][:].bitcast(U16).rearrange("p (m t) -> p t m", t=PACK),
             )
@@ -181,7 +181,10 @@ def tile_list_crop_index_payout_kernel(
             round_w1(1, w1_raw1, ts)
         for ts in (range(0, 2), range(2, 4)):
             quantize_w1(1, ts)
-        deal(w3_w[:], w3_raw[:])
+        nc.vector.tensor_copy(
+            out=w3_w[:].rearrange("p (a t m i) -> p a m t i", a=PASSES, t=PACK, i=4),
+            in_=w3_raw[:].rearrange("p (a m i t) -> p a m t i", a=PASSES, t=PACK, i=4),
+        )
         w4_bf = shared.tile([P, PACK * N], BF16, name="w4_bf", offset=AT_W4_BF, align_bytes=64)
 
         def first_stage(acc, first, width, codes, scales, order=(0, 1)):
@@ -210,8 +213,7 @@ def tile_list_crop_index_payout_kernel(
             place = block * BLOCK % CHUNK
             b = psum.tile([P, 2, BLOCK], F32, name="b", tag="b", bufs=4)
             for e in range(2):
-                for within in range(0, BLOCK, P):
-                    product_b(b[:, e, within : within + P], 2 * pair + e, block * BLOCK + within, P)
+                product_b(b[:, e, :], 2 * pair + e, block * BLOCK, BLOCK)
             nc.scalar.activation(b2[:, 2 * pair : 2 * pair + 2, place : place + BLOCK], b[:], ACT.Square)
 
         def banks(u):
@@ -296,13 +298,10 @@ def tile_list_crop_index_payout_kernel(
 
             for g in range(GROUPS):
                 negated_w4(gap[:, g, :], g, False)
-                for within in range(0, width, P):
-                    part = slice(first + within, first + within + P)
-                    nc.tensor.matmul_mx(
-                        out=gap[:, g, within : within + P], lhsT=w5_w[:, 2 * g * P : 2 * (g + 1) * P].bitcast(FP4X4),
-                        lhsT_scale=w5_s[:, g * P : (g + 1) * P],
-                        rhs=h_w[:, part].bitcast(FP8X4), rhs_scale=h_s[:, part], start=False, stop=(within + P == width),
-                    )
+                nc.tensor.matmul_mx(
+                    out=gap[:, g, :], lhsT=w5_w[:, 2 * g * P : 2 * (g + 1) * P].bitcast(FP4X4), lhsT_scale=w5_s[:, g * P : (g + 1) * P],
+                    rhs=h_w[:, cols].bitcast(FP8X4), rhs_scale=h_s[:, cols], start=False, stop=True,
+                )
             for g in range(GROUPS):
                 negated_w4(neg[:, g, :], g, True)
             if u == SHARED_UNIT:
@@ -325,7 +324,7 @@ def tile_list_crop_index_payout_kernel(
         overs = [keep.tile([P, GROUPS, WIDTHS[u]], F32, name="over%d" % u) for u in range(UNITS) if u != 3]
         overs.insert(3, shared.tile([P, GROUPS, WIDTHS[3]], F32, name="over3", offset=AT_OVER_3))
         scores = [keep.tile([P, GROUPS, WIDTHS[u]], F32, name="score%d" % u) for u in range(UNITS) if u not in (SHARED_UNIT, 2)]
-        scores.insert(SHARED_UNIT, shared.tile([P, GROUPS, BLOCK], F32, name="score_shared", offset=AT_SCORE))
+        scores.insert(SHARED_UNIT, keep.tile([P, GROUPS, BLOCK], F32, name="score_shared"))
         scores.insert(2, shared.tile([P, GROUPS, BLOCK], F32, name="score2", offset=AT_SCORE_2))
         h_blocks = [keep.tile([P, PACK, BLOCK], F32, name="h%d" % block) for block in range(BLOCKS)]
 

@@ -48,6 +48,7 @@ AT_W4_BF = AT_W3_RAW + 4096 - OVERLAP
 AT_H_BF = AT_W4_BF + 2048 - OVERLAP
 AT_SCORE = AT_H_BF + 3 * (2048 - OVERLAP)
 AT_H_BF_LATE = (AT_SCORE + 2048, AT_SCORE + 2048 + 1024 + 2048 - OVERLAP)
+AT_SCORE_PARTS = (AT_SCORE, AT_H_BF_LATE[0] - 1024 + OVERLAP)
 AT_SCORE_2 = AT_H_BF_LATE[0] + 1024
 AT_OVER_3 = AT_H_BF_LATE[1] + 1024 - OVERLAP
 AT_TAB_W1 = 40960
@@ -315,8 +316,7 @@ def tile_list_crop_index_payout_kernel(
             nc.vector.scalar_tensor_tensor(overs[u][:, groups, :], gap[:, groups, :], 0.0, ded_sb[:, groups, cols], ALU.max, ALU.subtract)
 
         def payout(u, neg, groups):
-            engine = nc.gpsimd if u == SHARED_UNIT else nc.vector
-            engine.tensor_tensor(scores[u][:, groups, :], overs[u][:, groups, :], neg[:, groups, :], ALU.subtract)
+            nc.vector.tensor_tensor(scores[u][:, groups, :], overs[u][:, groups, :], neg[:, groups, :], ALU.subtract)
 
         def store_scores(u):
             nc.sync.dma_start(out=out_0_rows[:, :, FIRSTS[u] : FIRSTS[u] + WIDTHS[u]], in_=scores[u][:])
@@ -324,7 +324,7 @@ def tile_list_crop_index_payout_kernel(
         overs = [keep.tile([P, GROUPS, WIDTHS[u]], F32, name="over%d" % u) for u in range(UNITS) if u != 3]
         overs.insert(3, shared.tile([P, GROUPS, WIDTHS[3]], F32, name="over3", offset=AT_OVER_3))
         scores = [keep.tile([P, GROUPS, WIDTHS[u]], F32, name="score%d" % u) for u in range(UNITS) if u not in (SHARED_UNIT, 2)]
-        scores.insert(SHARED_UNIT, keep.tile([P, GROUPS, BLOCK], F32, name="score_shared"))
+        scores.insert(SHARED_UNIT, None)
         scores.insert(2, shared.tile([P, GROUPS, BLOCK], F32, name="score2", offset=AT_SCORE_2))
         h_blocks = [keep.tile([P, PACK, BLOCK], F32, name="h%d" % block) for block in range(BLOCKS)]
 
@@ -383,8 +383,10 @@ def tile_list_crop_index_payout_kernel(
         sums.append(second_stage(4, rounded[4]))
         for q in range(QUADS):
             nc.scalar.dma_start(out=out_3[0, 4 * q : 4 * q + 4, :].bitcast(I32), in_=h_s[32 * q : 32 * q + 4, :].bitcast(I32))
-        payout(1, sums[1][1], both)
-        store_scores(1)
+        for g in range(GROUPS):
+            part = shared.tile([P, BLOCK], F32, name="score_shared%d" % g, offset=AT_SCORE_PARTS[g])
+            nc.gpsimd.tensor_tensor(part[:], overs[1][:, g, :], sums[1][1][:, g, :], ALU.subtract)
+            nc.sync.dma_start(out=out_0_rows[:, g, FIRSTS[1] : FIRSTS[1] + BLOCK], in_=part[:])
         payout(2, sums[2][1], both)
         store_scores(2)
         for u in (3, 4):

@@ -48,8 +48,7 @@ AT_W4_BF = AT_W3_RAW + 4096 - OVERLAP
 AT_H_BF = AT_W4_BF + 2048 - OVERLAP
 AT_SCORE = AT_H_BF + 3 * (2048 - OVERLAP)
 AT_H_BF_LATE = (AT_SCORE + 2048, AT_SCORE + 2048 + 1024 + 2048 - OVERLAP)
-AT_SCORE_PARTS = (AT_SCORE, AT_H_BF_LATE[0] - 1024 + OVERLAP)
-AT_SCORE_2 = AT_H_BF_LATE[0] + 1024
+AT_SCORE_LATE = AT_H_BF_LATE[1] - 3072 + OVERLAP
 AT_OVER_3 = AT_H_BF_LATE[1] + 1024 - OVERLAP
 AT_TAB_W1 = 40960
 AT_W4_RAW = AT_TAB_W1
@@ -325,7 +324,7 @@ def tile_list_crop_index_payout_kernel(
         overs.insert(3, shared.tile([P, GROUPS, WIDTHS[3]], F32, name="over3", offset=AT_OVER_3))
         scores = [keep.tile([P, GROUPS, WIDTHS[u]], F32, name="score%d" % u) for u in range(UNITS) if u not in (SHARED_UNIT, 2)]
         scores.insert(SHARED_UNIT, None)
-        scores.insert(2, shared.tile([P, GROUPS, BLOCK], F32, name="score2", offset=AT_SCORE_2))
+        scores.insert(2, None)
         h_blocks = [keep.tile([P, PACK, BLOCK], F32, name="h%d" % block) for block in range(BLOCKS)]
 
         damps = [[] for u in range(UNITS)]
@@ -383,12 +382,14 @@ def tile_list_crop_index_payout_kernel(
         sums.append(second_stage(4, rounded[4]))
         for q in range(QUADS):
             nc.scalar.dma_start(out=out_3[0, 4 * q : 4 * q + 4, :].bitcast(I32), in_=h_s[32 * q : 32 * q + 4, :].bitcast(I32))
-        for g in range(GROUPS):
-            part = shared.tile([P, BLOCK], F32, name="score_shared%d" % g, offset=AT_SCORE_PARTS[g])
-            nc.gpsimd.tensor_tensor(part[:], overs[1][:, g, :], sums[1][1][:, g, :], ALU.subtract)
-            nc.sync.dma_start(out=out_0_rows[:, g, FIRSTS[1] : FIRSTS[1] + BLOCK], in_=part[:])
-        payout(2, sums[2][1], both)
-        store_scores(2)
+        half = BLOCK // 2
+        early = shared.tile([P, GROUPS, half], F32, name="score_early", offset=AT_SCORE)
+        nc.gpsimd.tensor_tensor(early[:], overs[1][:, :, :half], sums[1][1][:, :, :half], ALU.subtract)
+        nc.sync.dma_start(out=out_0_rows[:, :, BLOCK : BLOCK + half], in_=early[:])
+        late = shared.tile([P, GROUPS, half + BLOCK], F32, name="score_late", offset=AT_SCORE_LATE)
+        nc.gpsimd.tensor_tensor(late[:, :, :half], overs[1][:, :, half:], sums[1][1][:, :, half:], ALU.subtract)
+        nc.vector.tensor_tensor(late[:, :, half:], overs[2][:], sums[2][1][:], ALU.subtract)
+        nc.sync.dma_start(out=out_0_rows[:, :, BLOCK + half : 3 * BLOCK], in_=late[:])
         for u in (3, 4):
             excess(u, sums[u][0], both)
         for u in (3, 4):

@@ -217,22 +217,21 @@ def tile_list_crop_index_payout_kernel(
             nc.scalar.activation(b2[:, 2 * pair : 2 * pair + 2, place : place + BLOCK], b[:], ACT.Square)
 
         def banks(u):
-            per = BANK // WIDTHS[u]
-            return [range(t, t + per) for t in range(0, PACK, per)]
+            return [range(0, 2), range(2, 4)]
 
         def denominator(u, ts, b2):
-            place, width = FIRSTS[u] % CHUNK, WIDTHS[u]
+            place, width = u * BLOCK % CHUNK, BLOCK
             den2 = ring.tile([P, len(ts), width], F32, name="den2", bufs=3)
             nc.scalar.activation(den2[:], b2[:, ts.start : ts.stop, place : place + width], ACT.Square, bias=bias_one[:])
             return den2
 
         def damping(u, ts, den2):
-            factor = keep.tile([P, len(ts), WIDTHS[u]], F32, name="damp%d_%d" % (u, ts.start))
+            factor = keep.tile([P, len(ts), BLOCK], F32, name="damp%d_%d" % (u, ts.start))
             nc.scalar.activation(factor[:], den2[:], ACT.Abs_reciprocal_sqrt)
             damps[u].append(factor)
 
         def damped_products(u):
-            first, width = FIRSTS[u], WIDTHS[u]
+            first, width = u * BLOCK, BLOCK
             acc_a, acc_c, damped = [], [], []
             for ts in banks(u):
                 acc_a.append(psum.tile([P, len(ts), width], F32, name="acc_a", tag="a"))
@@ -256,12 +255,14 @@ def tile_list_crop_index_payout_kernel(
             return damped, acc_c
 
         def features(u, damped, acc_c):
-            first, width = FIRSTS[u], WIDTHS[u]
-            block, place = divmod(first, BLOCK)
-            h = h_blocks[block][:, :, place : place + width]
+            cols = slice(u * BLOCK, (u + 1) * BLOCK)
+            h = h_blocks[u][:]
             for i, ts in enumerate(banks(u)):
                 nc.vector.tensor_tensor(h[:, ts.start : ts.stop, :], acc_c[i][:], damped[i][:], ALU.add)
-            nc.sync.dma_start(out=out_1_rows[:, :, first : first + width], in_=h)
+                if u == 3:
+                    nc.sync.dma_start(out=out_1_rows[:, ts.start : ts.stop, cols], in_=h[:, ts.start : ts.stop, :])
+            if u < 3:
+                nc.sync.dma_start(out=out_1_rows[:, :, cols], in_=h)
             return h
 
         def round_h(u, h):
@@ -274,10 +275,17 @@ def tile_list_crop_index_payout_kernel(
                 )
             else:
                 h_bf = shared.tile([P, PACK * width], BF16, name="h_bf%d" % u, offset=AT_H_BF_LATE[u - GPSIMD_UNITS], align_bytes=64)
-                nc.scalar.copy(
-                    out=h_bf[:].rearrange("p (m i t) -> p m t i", i=4, t=PACK), in_=h.rearrange("p t (m i) -> p m t i", i=4)
-                )
+                if u == 3:
+                    nc.scalar.copy(
+                        out=h_bf[:].rearrange("p (m i t) -> p m t i", i=4, t=PACK), in_=h.rearrange("p t (m i) -> p m t i", i=4)
+                    )
+                else:
+                    nc.gpsimd.tensor_scalar(
+                        h_bf[:].rearrange("p (m t) -> p m t", t=PACK), h.rearrange("p t m -> p m t"), 1.0, 0.0, ALU.mult, ALU.add
+                    )
             return h_bf
+
+        waiting = []
 
         def second_stage(u, h_bf):
             first, width = FIRSTS[u], WIDTHS[u]
@@ -302,8 +310,16 @@ def tile_list_crop_index_payout_kernel(
                     out=gap[:, g, :], lhsT=w5_w[:, 2 * g * P : 2 * (g + 1) * P].bitcast(FP4X4), lhsT_scale=w5_s[:, g * P : (g + 1) * P],
                     rhs=h_w[:, cols].bitcast(FP8X4), rhs_scale=h_s[:, cols], start=False, stop=True,
                 )
-            for g in range(GROUPS):
-                negated_w4(neg[:, g, :], g, True)
+            def minus_y1():
+                for g in range(GROUPS):
+                    negated_w4(neg[:, g, :], g, True)
+
+            if u == 3:
+                waiting.append(minus_y1)
+                return gap, neg
+            if u == 4:
+                waiting[0]()
+            minus_y1()
             if u == SHARED_UNIT:
                 neg_sb = keep.tile([P, GROUPS, width], F32, name="neg_sb")
                 nc.scalar.copy(neg_sb[:], neg[:])
@@ -349,10 +365,10 @@ def tile_list_crop_index_payout_kernel(
         square_b_block(3, 0, b2_late)
         damping(2, high, den_b)
         square_b_block(3, 1, b2_late)
-        den_a = denominator(3, banks(3)[0], b2_late)
-        den_b = denominator(4, banks(4)[0], b2_late)
-        damping(3, banks(3)[0], den_a)
-        damping(4, banks(4)[0], den_b)
+        den_a = denominator(3, low, b2_late)
+        den_b = denominator(3, high, b2_late)
+        damping(3, low, den_a)
+        damping(3, high, den_b)
 
         nc.gpsimd.tensor_scalar(
             w4_bf[:].rearrange("p (n j) -> p n j", j=PACK), w4_raw[:].rearrange("p j n -> p n j"), -1.0, 0.0, ALU.mult, ALU.add
@@ -373,19 +389,19 @@ def tile_list_crop_index_payout_kernel(
         rounded.append(round_h(2, h))
         parts = damped_products(3)
         excess(1, sums[1][0], both)
-        rounded.append(round_h(3, features(3, *parts)))
-        parts = damped_products(4)
         sums.append(second_stage(2, rounded[2]))
-        rounded.append(round_h(4, features(4, *parts)))
-        sums.append(second_stage(3, rounded[3]))
-        excess(2, sums[2][0], both)
-        sums.append(second_stage(4, rounded[4]))
-        for q in range(QUADS):
-            nc.scalar.dma_start(out=out_3[0, 4 * q : 4 * q + 4, :].bitcast(I32), in_=h_s[32 * q : 32 * q + 4, :].bitcast(I32))
         half = BLOCK // 2
         early = shared.tile([P, GROUPS, half], F32, name="score_early", offset=AT_SCORE)
         nc.gpsimd.tensor_tensor(early[:], overs[1][:, :, :half], sums[1][1][:, :, :half], ALU.subtract)
         nc.sync.dma_start(out=out_0_rows[:, :, BLOCK : BLOCK + half], in_=early[:])
+        h = features(3, *parts)
+        rounded.append(round_h(3, h[:, :, :half]))
+        rounded.append(round_h(4, h[:, :, half:]))
+        excess(2, sums[2][0], both)
+        sums.append(second_stage(3, rounded[3]))
+        sums.append(second_stage(4, rounded[4]))
+        for q in range(QUADS):
+            nc.scalar.dma_start(out=out_3[0, 4 * q : 4 * q + 4, :].bitcast(I32), in_=h_s[32 * q : 32 * q + 4, :].bitcast(I32))
         late = shared.tile([P, GROUPS, half + BLOCK], F32, name="score_late", offset=AT_SCORE_LATE)
         nc.gpsimd.tensor_tensor(late[:, :, :half], overs[1][:, :, half:], sums[1][1][:, :, half:], ALU.subtract)
         nc.vector.tensor_tensor(late[:, :, half:], overs[2][:], sums[2][1][:], ALU.subtract)

from contextlib import ExitStack

import concourse.mybir as mybir

K, H, N, T, S = 1024, 512, 256, 2048, 1024
FLOPS = 2 * S * H * (3 * K + 2 * N)

F32 = mybir.dt.float32
BF16 = mybir.dt.bfloat16
I32 = mybir.dt.int32
U32 = mybir.dt.uint32
U16 = mybir.dt.uint16
U8 = mybir.dt.uint8
FP8X4 = mybir.dt.float8_e4m3fn_x4
FP4X4 = mybir.dt.float4_e2m1fn_x4
ACT = mybir.ActivationFunctionType
ALU = mybir.AluOpType

P = 128
PACK = 4
PASSES = K // (P * PACK)
QUADS = 4
LIST_ROWS = 16
BANK = 512
CHUNK = 512
CHUNKS = S // CHUNK
BLOCK = 256
BLOCKS = S // BLOCK
PAIRS = PACK // 2
GROUPS = N // P

WIDTHS = [BLOCK, BLOCK, BLOCK, BLOCK // 2, BLOCK // 2]
FIRSTS = [sum(WIDTHS[:u]) for u in range(len(WIDTHS))]
UNITS = len(WIDTHS)
GPSIMD_UNITS = 3
SHARED_UNIT = 1
CODE_STORES = {512: 0, 768: 512, 1024: 768}

OVERLAP = 64
AT_W1_RAW0 = 0
AT_TAB_S = 7168
AT_W3_ROWS = 8192
AT_W1_RAW1 = 9216
AT_W2_RAW = 16896
AT_W2_S = 17408
AT_W3_RAW = 18432
AT_W4_BF = AT_W3_RAW + 4096 - OVERLAP
AT_H_BF = AT_W4_BF + 2048 - OVERLAP
AT_SCORE = AT_H_BF + 3 * (2048 - OVERLAP)
AT_H_BF_LATE = (AT_SCORE + 2048, AT_SCORE + 2048 + 1024 + 2048 - OVERLAP)
AT_SCORE_LATE = AT_H_BF_LATE[1] - 3072 + OVERLAP
AT_OVER_3 = AT_H_BF_LATE[1] + 1024 - OVERLAP
AT_TAB_W1 = 40960
AT_W4_RAW = AT_TAB_W1
AT_W5_W = AT_W4_RAW + 4096
AT_DED = AT_W5_W + 512


def tile_list_crop_index_payout_kernel(
    tc, tab_words, tab_scales, offs, w1, w2_words, w2_scales, w3_words, w3_scales, w4, w5_words, w5_scales, ded,
    out_0, out_1, out_2, out_3,
):
    nc = tc.nc
    with ExitStack() as ctx:
        keep = ctx.enter_context(tc.tile_pool(name="keep", bufs=1))
        shared = ctx.enter_context(tc.tile_pool(name="shared", bufs=1))
        ring = ctx.enter_context(tc.tile_pool(name="ring", bufs=2))
        psum = ctx.enter_context(tc.psum_pool(name="psum", bufs=2))

        offsets = keep.tile([P, S // LIST_ROWS], U16, name="offsets")
        tab_w = [
            keep.tile([P, T], I32, name="tab_w0", align_bytes=64),
            shared.tile([P, T], I32, name="tab_w1", offset=AT_TAB_W1, align_bytes=64),
        ]
        tab_s = shared.tile([P, T], U8, name="tab_s", offset=AT_TAB_S, align_bytes=64)
        v_w = [[keep.tile([P, CHUNK], U32, name="v_w%d_%d" % (a, c), align_bytes=64) for c in range(CHUNKS)] for a in range(PASSES)]
        picked_rows = keep.tile([P, S], U8, name="picked_rows", align_bytes=64)
        v_s = keep.tile([P, PASSES * S], U8, name="v_s", align_bytes=64)
        w1_bf = [keep.tile([P, PACK * H], BF16, name="w1_bf%d" % a, align_bytes=64) for a in range(PASSES)]
        w1_w = [keep.tile([P, H], U32, name="w1_w%d" % a, align_bytes=64) for a in range(PASSES)]
        w1_s = [keep.tile([P, H], U8, name="w1_s%d" % a, align_bytes=64) for a in range(PASSES)]
        w2_raw = [shared.tile([P, 2 * H], U8, name="w2_raw%d" % a, offset=AT_W2_RAW + 2 * H * a, align_bytes=64) for a in range(PASSES)]
        w2_w = keep.tile([P, PASSES * 2 * H], U8, name="w2_w", align_bytes=64)
        w3_w = keep.tile([P, PASSES * H], I32, name="w3_w", align_bytes=64)
        w2_rows = keep.tile([P, PASSES * H], U8, name="w2_rows", align_bytes=64)
        w2_s = keep.tile([P, PASSES * H], U8, name="w2_s", align_bytes=64)
        w3_s = keep.tile([P, H], U8, name="w3_s", align_bytes=64)
        w4_w = keep.tile([P, N], U32, name="w4_w", align_bytes=64)
        w4_s = keep.tile([P, N], U8, name="w4_s", align_bytes=64)
        out_1_rows = out_1.rearrange("(p t) s -> p t s", t=PACK)
        out_0_rows = out_0.rearrange("(g p) s -> p g s", p=P)
        h_w = keep.tile([P, S], U32, name="h_w", align_bytes=64)
        h_s = keep.tile([P, S], U8, name="h_s", align_bytes=64)
        unity = keep.tile([P, 1], F32, name="unity")
        bias_one = keep.tile([P, 1], F32, name="bias_one")

        nc.gpsimd.memset(w2_rows[:].bitcast(I32), 0)
        nc.gpsimd.memset(v_s[:].bitcast(I32), 0)
        nc.vector.memset(unity[:], 1.0)
        for rows in (tab_s[32:64, :], tab_s[64:P, :]):
            nc.vector.memset(rows.bitcast(I32), 0)

        def words(dram, a):
            return dram[a].rearrange("p e i -> p (e i)").bitcast(I32)

        nc.sync.dma_start(offsets[:], offs)
        nc.sync.dma_start(out=tab_s[0:32, :].bitcast(I32), in_=tab_scales.bitcast(I32).rearrange("a q t -> q a t"))
        for a in range(PASSES):
            nc.sync.dma_start(out=tab_w[a][:], in_=words(tab_words, a))
            nc.sync.dma_start(out=w2_raw[a][:].bitcast(I32), in_=w2_words[a].bitcast(I32))
        for q in range(QUADS):
            nc.scalar.dma_start(
                out=w2_rows[32 * q : 32 * q + 4, :].bitcast(I32).rearrange("r (a e) -> r a e", a=PASSES),
                in_=w2_scales.bitcast(I32)[:, 4 * q : 4 * q + 4, :].rearrange("a r e -> r a e"),
            )
        nc.scalar.activation(bias_one[:], unity[:], ACT.Abs_reciprocal_sqrt)

        def load_w1(a, at):
            raw = shared.tile([P, PACK, H], F32, name="w1_raw%d" % a, offset=at, align_bytes=64)
            nc.sync.dma_start(out=raw[:], in_=w1[P * PACK * a : P * PACK * (a + 1), :].rearrange("(p j) r -> p j r", j=PACK))
            return raw

        def deal(dst, src):
            nc.vector.tensor_copy(
                out=dst.rearrange("p (a t m) -> p a m t", m=P, t=PACK), in_=src.rearrange("p (a m t) -> p a m t", m=P, t=PACK)
            )

        def round_w1(a, raw, ts):
            nc.vector.tensor_copy(
                out=w1_bf[a][:].rearrange("p (t m j) -> p m j t", t=PACK, j=PACK)[:, :, :, ts.start : ts.stop],
                in_=raw[:].rearrange("p j (m t) -> p m j t", t=PACK)[:, :, :, ts.start : ts.stop],
            )

        def quantize_w1(a, ts):
            cols = slice(P * ts.start, P * ts.stop)
            nc.vector.quantize_mx(
                out=w1_w[a][:, cols].bitcast(FP8X4), scales=w1_s[a][:, cols], in_=w1_bf[a][:, PACK * cols.start : PACK * cols.stop]
            )

        nc.vector.tensor_copy(picked_rows[:], tab_s[:].indirect(offsets[:]))

        for q in range(QUADS):
            nc.sync.dma_start(
                out=v_s[32 * q : 32 * q + 4, :].bitcast(I32).rearrange("r (a s) -> r a s", a=PASSES),
                in_=picked_rows[8 * q : 8 * q + 8, :].bitcast(I32),
            )
        w1_raw0 = load_w1(0, AT_W1_RAW0)
        nc.gpsimd.tensor_copy(
            out=w2_s[:].rearrange("p (a t m) -> p a t m", m=P, t=PACK), in_=w2_rows[:].rearrange("p (a m t) -> p a t m", m=P, t=PACK)
        )
        for a in range(PASSES):
            nc.scalar.copy(
                out=w2_w[:, 2 * H * a : 2 * H * (a + 1)].bitcast(U16).rearrange("p (t m) -> p t m", t=PACK),
                in_=w2_raw[a][:].bitcast(U16).rearrange("p (m t) -> p t m", t=PACK),
            )
        w3_rows = w2_rows[:, 0:H]
        for q in range(QUADS):
            nc.sync.dma_start(out=w3_rows[32 * q + 4 : 32 * q + 12, :].bitcast(I32), in_=w3_scales.bitcast(I32)[:, 4 * q : 4 * q + 4, :])
        for a, c in ((0, 0), (0, 1), (1, 0), (1, 1)):
            part = offsets[:, c * CHUNK // LIST_ROWS : (c + 1) * CHUNK // LIST_ROWS]
            nc.vector.tensor_copy(v_w[a][c][:], tab_w[a][:].bitcast(U32).indirect(part))
        w1_raw1 = load_w1(1, AT_W1_RAW1)
        w3_raw = shared.tile([P, PASSES * H], I32, name="w3_raw", offset=AT_W3_RAW, align_bytes=64)
        nc.sync.dma_start(
            out=w3_raw[:].rearrange("p (a e) -> p a e", a=PASSES),
            in_=w3_words.rearrange("a p e i -> a p (e i)").bitcast(I32).rearrange("a p e -> p a e"),
        )
        w4_raw = shared.tile([P, PACK, N], F32, name="w4_raw", offset=AT_W4_RAW, align_bytes=64)
        nc.sync.dma_start(out=w4_raw[:], in_=w4.rearrange("(p j) n -> p j n", j=PACK))
        w5_w = shared.tile([P, 2 * N], U8, name="w5_w", offset=AT_W5_W, align_bytes=64)
        nc.sync.dma_start(out=w5_w[:].bitcast(I32), in_=w5_words[0].bitcast(I32))
        ded_sb = shared.tile([P, GROUPS, S], F32, name="ded_sb", offset=AT_DED, align_bytes=64)
        nc.sync.dma_start(out=ded_sb[:], in_=ded.rearrange("(g p) s -> p g s", p=P))
        round_w1(0, w1_raw0, range(PACK))
        deal(w3_s[:], w3_rows)
        quantize_w1(0, range(PACK))
        w5_s = w3_rows[:, 0:N]
        for q in range(QUADS):
            nc.sync.dma_start(out=w5_s[32 * q : 32 * q + 4, :].bitcast(I32), in_=w5_scales[0, 4 * q : 4 * q + 4, :].bitcast(I32))
        for ts in (range(0, 2), range(2, 4)):
            round_w1(1, w1_raw1, ts)
        for ts in (range(0, 2), range(2, 4)):
            quantize_w1(1, ts)
        nc.vector.tensor_copy(
            out=w3_w[:].rearrange("p (a t m i) -> p a m t i", a=PASSES, t=PACK, i=4),
            in_=w3_raw[:].rearrange("p (a m i t) -> p a m t i", a=PASSES, t=PACK, i=4),
        )
        w4_bf = shared.tile([P, PACK * N], BF16, name="w4_bf", offset=AT_W4_BF, align_bytes=64)

        def first_stage(acc, first, width, codes, scales, order=(0, 1)):
            c, within = divmod(first, CHUNK)
            for a in order:
                nc.tensor.matmul_mx(
                    out=acc, lhsT=codes(a), lhsT_scale=scales(a), rhs=v_w[a][c][:, within : within + width].bitcast(FP8X4),
                    rhs_scale=v_s[:, a * S + first : a * S + first + width], start=(a == order[0]), stop=(a == order[-1]),
                )

        def product_b(acc, t, first, width, order=(0, 1)):
            first_stage(
                acc, first, width,
                lambda a: w2_w[:, 2 * (a * H + t * P) : 2 * (a * H + (t + 1) * P)].bitcast(FP4X4),
                lambda a: w2_s[:, a * H + t * P : a * H + (t + 1) * P],
                order,
            )

        def square_b_chunk(c, ts, b2):
            for t in ts:
                b = psum.tile([P, CHUNK], F32, name="b", tag="b", bufs=4)
                product_b(b[:], t, c * CHUNK, CHUNK, (0, 1) if t == 0 else (1, 0))
                nc.scalar.activation(b2[:, t, :], b[:], ACT.Square)

        def square_b_block(block, pair, b2):
            place = block * BLOCK % CHUNK
            b = psum.tile([P, 2, BLOCK], F32, name="b", tag="b", bufs=4)
            for e in range(2):
                product_b(b[:, e, :], 2 * pair + e, block * BLOCK, BLOCK)
            nc.scalar.activation(b2[:, 2 * pair : 2 * pair + 2, place : place + BLOCK], b[:], ACT.Square)

        def banks(u):
            return [range(0, 2), range(2, 4)]

        def denominator(u, ts, b2):
            place, width = u * BLOCK % CHUNK, BLOCK
            den2 = ring.tile([P, len(ts), width], F32, name="den2", bufs=3)
            nc.scalar.activation(den2[:], b2[:, ts.start : ts.stop, place : place + width], ACT.Square, bias=bias_one[:])
            return den2

        def damping(u, ts, den2):
            factor = keep.tile([P, len(ts), BLOCK], F32, name="damp%d_%d" % (u, ts.start))
            nc.scalar.activation(factor[:], den2[:], ACT.Abs_reciprocal_sqrt)
            damps[u].append(factor)

        def damped_products(u):
            first, width = u * BLOCK, BLOCK
            acc_a, acc_c, damped = [], [], []
            for ts in banks(u):
                acc_a.append(psum.tile([P, len(ts), width], F32, name="acc_a", tag="a"))
                for t in ts:
                    first_stage(
                        acc_a[-1][:, t - ts.start, :], first, width,
                        lambda a: w1_w[a][:, t * P : (t + 1) * P].bitcast(FP8X4),
                        lambda a: w1_s[a][:, t * P : (t + 1) * P],
                    )
            for ts in banks(u):
                acc_c.append(psum.tile([P, len(ts), width], F32, name="acc_c", tag="c"))
                for t in ts:
                    first_stage(
                        acc_c[-1][:, t - ts.start, :], first, width,
                        lambda a: w3_w[:, a * H + t * P : a * H + (t + 1) * P].bitcast(FP8X4),
                        lambda a: w3_s[4 * a + 4 : P, t * P : (t + 1) * P],
                    )
            for i, ts in enumerate(banks(u)):
                damped.append(ring.tile([P, len(ts), width], F32, name="damped"))
                nc.vector.tensor_tensor(damped[i][:], acc_a[i][:], damps[u][i][:], ALU.mult)
            return damped, acc_c

        def features(u, damped, acc_c):
            cols = slice(u * BLOCK, (u + 1) * BLOCK)
            h = h_blocks[u][:]
            for i, ts in enumerate(banks(u)):
                nc.vector.tensor_tensor(h[:, ts.start : ts.stop, :], acc_c[i][:], damped[i][:], ALU.add)
                if u == 3:
                    nc.sync.dma_start(out=out_1_rows[:, ts.start : ts.stop, cols], in_=h[:, ts.start : ts.stop, :])
            if u < 3:
                nc.sync.dma_start(out=out_1_rows[:, :, cols], in_=h)
            return h

        def round_h(u, h):
            width = WIDTHS[u]
            if u < GPSIMD_UNITS:
                at = AT_H_BF + (2 * PACK * BLOCK - OVERLAP) * u
                h_bf = shared.tile([P, PACK * width], BF16, name="h_bf%d" % u, offset=at, align_bytes=64)
                nc.gpsimd.tensor_scalar(
                    h_bf[:].rearrange("p (m t) -> p m t", t=PACK), h.rearrange("p t m -> p m t"), 1.0, 0.0, ALU.mult, ALU.add
                )
            else:
                h_bf = shared.tile([P, PACK * width], BF16, name="h_bf%d" % u, offset=AT_H_BF_LATE[u - GPSIMD_UNITS], align_bytes=64)
                if u == 3:
                    nc.scalar.copy(
                        out=h_bf[:].rearrange("p (m i t) -> p m t i", i=4, t=PACK), in_=h.rearrange("p t (m i) -> p m t i", i=4)
                    )
                else:
                    nc.gpsimd.tensor_scalar(
                        h_bf[:].rearrange("p (m t) -> p m t", t=PACK), h.rearrange("p t m -> p m t"), 1.0, 0.0, ALU.mult, ALU.add
                    )
            return h_bf

        waiting = []

        def second_stage(u, h_bf):
            first, width = FIRSTS[u], WIDTHS[u]
            cols = slice(first, first + width)
            nc.vector.quantize_mx(out=h_w[:, cols].bitcast(FP8X4), scales=h_s[:, cols], in_=h_bf[:])
            if first + width in CODE_STORES:
                done = slice(CODE_STORES[first + width], first + width)
                nc.sync.dma_start(out=words(out_2, 0)[:, done], in_=h_w[:, done].bitcast(I32))
            tag, bufs = {3: ("a", 2), 4: ("c", 2)}.get(u, ("b", 4))
            gap = psum.tile([P, GROUPS, width], F32, name="gap", tag=tag, bufs=bufs)
            neg = psum.tile([P, GROUPS, width], F32, name="neg", tag=tag, bufs=bufs)

            def negated_w4(acc, g, stop):
                nc.tensor.matmul_mx(
                    out=acc, lhsT=w4_w[:, g * P : (g + 1) * P].bitcast(FP8X4), lhsT_scale=w4_s[:, g * P : (g + 1) * P],
                    rhs=h_w[:, cols].bitcast(FP8X4), rhs_scale=h_s[:, cols], start=True, stop=stop,
                )

            for g in range(GROUPS):
                negated_w4(gap[:, g, :], g, False)
                nc.tensor.matmul_mx(
                    out=gap[:, g, :], lhsT=w5_w[:, 2 * g * P : 2 * (g + 1) * P].bitcast(FP4X4), lhsT_scale=w5_s[:, g * P : (g + 1) * P],
                    rhs=h_w[:, cols].bitcast(FP8X4), rhs_scale=h_s[:, cols], start=False, stop=True,
                )
            def minus_y1():
                for g in range(GROUPS):
                    negated_w4(neg[:, g, :], g, True)

            if u == 3:
                waiting.append(minus_y1)
                return gap, neg
            if u == 4:
                waiting[0]()
            minus_y1()
            if u == SHARED_UNIT:
                neg_sb = keep.tile([P, GROUPS, width], F32, name="neg_sb")
                nc.scalar.copy(neg_sb[:], neg[:])
                return gap, neg_sb
            return gap, neg

        def excess(u, gap, groups):
            cols = slice(FIRSTS[u], FIRSTS[u] + WIDTHS[u])
            nc.vector.scalar_tensor_tensor(overs[u][:, groups, :], gap[:, groups, :], 0.0, ded_sb[:, groups, cols], ALU.max, ALU.subtract)

        def payout(u, neg, groups):
            nc.vector.tensor_tensor(scores[u][:, groups, :], overs[u][:, groups, :], neg[:, groups, :], ALU.subtract)

        def store_scores(u):
            nc.sync.dma_start(out=out_0_rows[:, :, FIRSTS[u] : FIRSTS[u] + WIDTHS[u]], in_=scores[u][:])

        overs = [keep.tile([P, GROUPS, WIDTHS[u]], F32, name="over%d" % u) for u in range(UNITS) if u != 3]
        overs.insert(3, shared.tile([P, GROUPS, WIDTHS[3]], F32, name="over3", offset=AT_OVER_3))
        scores = [keep.tile([P, GROUPS, WIDTHS[u]], F32, name="score%d" % u) for u in range(UNITS) if u not in (SHARED_UNIT, 2)]
        scores.insert(SHARED_UNIT, None)
        scores.insert(2, None)
        h_blocks = [keep.tile([P, PACK, BLOCK], F32, name="h%d" % block) for block in range(BLOCKS)]

        damps = [[] for u in range(UNITS)]
        low, high = banks(0)
        b2_early = keep.tile([P, PACK, CHUNK], F32, name="b2_early")
        b2_late = keep.tile([P, PACK, CHUNK], F32, name="b2_late")
        square_b_chunk(0, range(0, 3), b2_early)
        den_a = denominator(0, low, b2_early)
        square_b_chunk(0, range(3, 4), b2_early)
        damping(0, low, den_a)
        den_b = denominator(0, high, b2_early)
        den_a = denominator(1, low, b2_early)
        damping(0, high, den_b)
        den_b = denominator(1, high, b2_early)
        damping(1, low, den_a)
        square_b_block(2, 0, b2_late)
        damping(1, high, den_b)
        square_b_block(2, 1, b2_late)
        den_a = denominator(2, low, b2_late)
        den_b = denominator(2, high, b2_late)
        damping(2, low, den_a)
        square_b_block(3, 0, b2_late)
        damping(2, high, den_b)
        square_b_block(3, 1, b2_late)
        den_a = denominator(3, low, b2_late)
        den_b = denominator(3, high, b2_late)
        damping(3, low, den_a)
        damping(3, high, den_b)

        nc.gpsimd.tensor_scalar(
            w4_bf[:].rearrange("p (n j) -> p n j", j=PACK), w4_raw[:].rearrange("p j n -> p n j"), -1.0, 0.0, ALU.mult, ALU.add
        )
        both = slice(0, GROUPS)
        h = features(0, *damped_products(0))
        nc.vector.quantize_mx(out=w4_w[:].bitcast(FP8X4), scales=w4_s[:], in_=w4_bf[:])
        rounded = [round_h(0, h)]
        h = features(1, *damped_products(1))
        sums = [second_stage(0, rounded[0])]
        rounded.append(round_h(1, h))
        parts = damped_products(2)
        excess(0, sums[0][0], both)
        h = features(2, *parts)
        sums.append(second_stage(1, rounded[1]))
        payout(0, sums[0][1], both)
        store_scores(0)
        rounded.append(round_h(2, h))
        parts = damped_products(3)
        excess(1, sums[1][0], both)
        sums.append(second_stage(2, rounded[2]))
        half = BLOCK // 2
        early = shared.tile([P, GROUPS, half], F32, name="score_early", offset=AT_SCORE)
        nc.gpsimd.tensor_tensor(early[:], overs[1][:, :, :half], sums[1][1][:, :, :half], ALU.subtract)
        nc.sync.dma_start(out=out_0_rows[:, :, BLOCK : BLOCK + half], in_=early[:])
        h = features(3, *parts)
        rounded.append(round_h(3, h[:, :, :half]))
        rounded.append(round_h(4, h[:, :, half:]))
        excess(2, sums[2][0], both)
        sums.append(second_stage(3, rounded[3]))
        sums.append(second_stage(4, rounded[4]))
        for q in range(QUADS):
            nc.scalar.dma_start(out=out_3[0, 4 * q : 4 * q + 4, :].bitcast(I32), in_=h_s[32 * q : 32 * q + 4, :].bitcast(I32))
        late = shared.tile([P, GROUPS, half + BLOCK], F32, name="score_late", offset=AT_SCORE_LATE)
        nc.gpsimd.tensor_tensor(late[:, :, :half], overs[1][:, :, half:], sums[1][1][:, :, half:], ALU.subtract)
        nc.vector.tensor_tensor(late[:, :, half:], overs[2][:], sums[2][1][:], ALU.subtract)
        nc.sync.dma_start(out=out_0_rows[:, :, BLOCK + half : 3 * BLOCK], in_=late[:])
        for u in (3, 4):
            excess(u, sums[u][0], both)
        for u in (3, 4):
            payout(u, sums[u][1], both)
            store_scores(u)
